import numpy as np, ml_dtypes
CORES = [25,29,65,69,153,157,193,197]
N = 8
import mx_ref
BF = ml_dtypes.bfloat16
def entries(a):
    return np.ascontiguousarray(a.T).reshape(-1)
def table(e):
    return np.ascontiguousarray(np.reshape(e, (-1, 16)).T).astype(np.int32)
def gentries(a):
    return np.ascontiguousarray(a.reshape(8, 16, -1).transpose(0, 2, 1)).reshape(8, -1)
def gtable(e):
    e = np.asarray(e); return np.ascontiguousarray(e.reshape(8, -1, 16).transpose(0, 2, 1)).reshape(128, -1).astype(np.int32)
def tile(rs):
    return np.stack(rs, axis=2).reshape(128, -1).astype(BF)
def pick(q, e):
    c = np.concatenate([q[0].reshape(128, -1, 4), np.zeros((128, 1, 4), np.uint8)], axis=1); s = np.concatenate([q[1], np.ones((16, 1), np.uint8)], axis=1)
    return (np.ascontiguousarray(c[:, e].reshape(128, -1)), np.ascontiguousarray(s[:, e]))
def join(*qs):
    return (np.concatenate([q[0] for q in qs], axis=1), np.concatenate([q[1] for q in qs], axis=1))
def put(q, e, v):
    c, s = q[0].reshape(128, -1, 4).copy(), q[1].copy(); c[:, e] = v[0].reshape(128, -1, 4); s[:, e] = v[1]
    return (c.reshape(128, -1), s)
def pk(c, s):
    return (np.ascontiguousarray(c), mx_ref.live(s))
def emit(q):
    return q[0], q[1]
def packed(v, rng):
    q = [mx_ref.quantize(np.ascontiguousarray(v[r])) for r in range(N)]
    return np.stack([a for a, b in q]), np.stack([mx_ref.plane(b, rng) for a, b in q])
def values_of_codes():
    e, c = np.zeros((128, 128, 4), np.float32), np.zeros((128, 2, 4), np.uint8)
    e[np.arange(128), np.arange(128), 0] = 1
    c[:127, :, 0] = np.arange(256).reshape(2, 128).T[:127]
    return mx_ref.matmul(mx_ref.quantize(e.reshape(128, 512).astype(BF)), (c.reshape(128, 8), np.full((16, 2), 127, np.uint8))).T.reshape(-1).astype(np.float64)
CODE_VALUE, SCALE_VALUE = values_of_codes(), 2.0 ** (np.arange(256) - 127.0)
def decode(q):
    return (CODE_VALUE[q[0]].reshape(16, 8, -1, 4) * SCALE_VALUE[q[1]][:, None, :, None] + 0.0).reshape(128, -1).astype(np.float32)
def f(rng, *shape):
    return mx_ref.flush((rng.standard_normal(shape, dtype=np.float32) * np.exp2(rng.integers(-2, 3, shape[:-1] + (1,)))).astype(BF))
def wide(rng, *shape, cols=0):
    v = rng.standard_normal(shape, dtype=np.float32) * np.exp2(rng.integers(-12, 13, shape)).astype(np.float32)
    if cols: v *= np.repeat(np.exp2(rng.integers(-cols, cols + 1, shape[:-2] + (1, shape[-1] // 4))) * (rng.random(shape[:-2] + (1, shape[-1] // 4)) > 0.0625), 4, axis=-1).astype(np.float32)
    return mx_ref.flush(v.astype(BF))
C, T, K, STEPS = 400, 320, 96, 3
MATES = [1, 2, 4]
DECIDE = [16 * i + k for i in range(STEPS) for k in range(2)]
def numbers_of(rng):
    return {"x": np.array(f(rng, N, 128, 4 * C)), "u": np.array(f(rng, N, 128, 512)), "v": np.array(f(rng, N, 128, 512))}
def lists(rng):
    return {"p": np.stack([gtable(np.stack([rng.permutation(C) for g in range(8)])) for r in range(N)]),
            "ln": np.stack([table(np.concatenate([rng.permutation(T) for i in range(STEPS)])) for r in range(N)])}
def layers(rng):
    k = np.exp2(rng.permuted(np.tile(np.arange(128) % 5 - 2.0, (N, 1)), axis=1))[:, :, None]
    return np.array(mx_ref.flush((rng.standard_normal((N, 128, 2048)) * k).astype(np.float32).astype(BF))).reshape(N, 8, 16, 4, 8, 16, 4)
def weights(rng, w):
    c, s = packed(np.ascontiguousarray(w).reshape(N, 128, 2048), rng)
    return {"wc": c, "ws": s}
def setup_inputs(rng):
    return {**numbers_of(rng), **lists(rng), **weights(rng, layers(rng))}
def setup_inputs_ties(rng):
    d = numbers_of(rng)
    x = d["x"].reshape(N, 8, 16, C, 4)
    x[:, :, 0] = 0
    x[:, :, 0, :, 0] = rng.integers(-1, 2, (N, 8, C)).astype(np.float32).astype(BF)
    x[:, :, :, ::8] = 0
    u = d["u"].reshape(N, 128, 128, 4)
    u[:, :, DECIDE] = 0
    o = rng.permutation(N)
    for r in range(N):
        g = rng.permutation(8)
        for i, c in enumerate(DECIDE): u[r, 16 * g[i], c, 0] = 0.0 if r == o[0] else -1.0 if r == o[1] else 1.0
    w = layers(rng)
    w[:, :, 0] = 0
    w[:, :, :, :, :, 0] = 0
    return {"x": x.reshape(N, 128, 4 * C), "u": u.reshape(N, 128, 512), "v": d["v"], **lists(rng), **weights(rng, w)}
def setup_inputs_near(rng):
    d = numbers_of(rng)
    x = d["x"].reshape(N, 8, 16, C, 4)
    u = d["u"].reshape(N, 128, 128, 4)
    x[:, :, :8] = 0
    u[:, :, DECIDE] = 0
    o = rng.permutation(N)
    for r in range(N):
        k = 2.0 ** -30 if o[r] % 2 == 0 else 1.0
        s = rng.integers(-1, 2, (8, C)) * k
        x[r, :, 0, :, 0] = (1.125 * s).astype(np.float32).astype(BF)
        x[r, :, 1, :, 0] = (-s).astype(np.float32).astype(BF)
        for g in rng.permutation(8)[:4]:
            c = rng.integers(T)
            x[r, g, 0, c, 0] = 2.0 ** 16 * rng.choice([-1.0, 1.0])
            x[r, g, 1, c, 0] = 0
        g = rng.permutation(8)
        for i, c in enumerate(DECIDE):
            u[r, 16 * g[i], c, 0] = 1.125 * k
            u[r, 16 * g[i] + 1, c, 0] = 1.25 * k
    w = layers(rng)
    w[:, :, :8] = 0
    w[:, :, :, :, :, :8] = 0
    return {"x": x.reshape(N, 128, 4 * C), "u": u.reshape(N, 128, 512), "v": d["v"], **lists(rng), **weights(rng, w)}
def setup_inputs_twice(rng):
    d = numbers_of(rng)
    x = d["x"].reshape(N, 8, 16, C, 4)
    a = (2 * rng.integers(2, 8, (N, 8, 8, C, 4)) + 1) * np.exp2(rng.integers(-5, -3, (N, 8, 8, C, 4)))
    a[:, :, 0, :, 0] = 1.96875 * 2.0 ** 12
    x[:, :, :8] = (a * rng.choice([-1.0, 1.0], a.shape)).astype(np.float32).astype(BF)
    w = layers(rng)
    w[:, :, 0] = 0
    w[:, :, :, :, :, :8] = 0
    return {"x": x.reshape(N, 128, 4 * C), "u": d["u"], "v": d["v"], **lists(rng), **weights(rng, w)}
def setup_inputs_ends(rng):
    d = numbers_of(rng)
    e = rng.permutation(N) % 4
    x, w = np.zeros((N, 8, 16, C, 4)), np.zeros((N, 128, 4, 128, 4), np.float32)
    u = d["u"].reshape(N, 128, 128, 4)
    v, p, n, j, i = [], [], [], np.arange(C), np.arange(128)
    for r in range(N):
        k = e[r]
        s = rng.choice([-1.0, 1.0], (8, 1, C, 1))
        x[r] = 2.0 ** 17 * (1.0, s[:1], 2.0 ** -47, s)[k]
        for c in DECIDE:
            a = (2.0 ** 30, 0.0, 2.0 ** -30 if c % 16 else -2.0 ** -30, 2.0 ** 30 * rng.choice([-1.0, 1.0], (128, 4)))[k]
            u[r, :, c] = np.asarray(a, np.float32).astype(BF)
        v.append((1.0 if k == 0 else rng.choice([-1.0, 1.0], (128, 512))) * np.full((128, 512), 2.0 ** (-30 if k == 2 else 30)))
        if k == 3:
            for b in range(4): w[r, (i + 16) % 128, b, i, b] = -1024
        else: w[r] = (2, 0, -2)[k]
        p.append(gtable((np.tile(j, (8, 1)), np.tile(j[::-1], (8, 1)), (j + 16 * np.arange(8)[:, None] + 1) % C, np.stack([rng.permutation(C) for g in range(8)]))[k]))
        n.append(table((np.tile(np.arange(T), STEPS), np.tile(np.arange(T)[::-1], STEPS), np.tile(rng.permutation(T), STEPS), np.concatenate([rng.permutation(T) for g in range(STEPS)]))[k]))
    return {"x": x.astype(np.float32).reshape(N, 128, 4 * C).astype(BF), "u": u.reshape(N, 128, 512), "v": np.stack(v).astype(np.float32).astype(BF), "p": np.stack(p), "ln": np.stack(n), **weights(rng, w.astype(BF))}
def setup_inputs_spread(rng):
    d = setup_inputs(rng)
    d["x"] = wide(rng, N, 128, 4 * C, cols=2)
    return d
def check_inputs(d):
    b = []
    for k, most in (("x", 2.0 ** 17), ("u", 2.0 ** 30), ("v", 2.0 ** 30)):
        a = np.abs(d[k].astype(np.float32))
        if not (np.isfinite(a).all() and ((a == 0) | (a >= 2.0 ** -30) & (a <= most)).all()): b.append("a value of " + k)
    none, least, most = [emit(mx_ref.quantize(np.full((128, 16), k, np.float32).astype(BF)))[1][0, 0] for k in (0.0, 2.0 ** -30, 2.0 ** 30)]
    for r in range(N):
        if (np.sort(gentries(d["p"][r]), axis=1) != np.arange(C)).any(): b.append("p: a group's entries aren't a permutation")
        if (np.sort(entries(d["ln"][r]).reshape(STEPS, T), axis=1) != np.arange(T)).any(): b.append("ln: a step's entries aren't a permutation")
        if ((d["wc"][r] & 0x7F) == 0x7F).any(): b.append("wc: a code that is no number")
        s = mx_ref.live(d["ws"][r])
        if ((s != none) & ((s < least) | (s > most))).any(): b.append("ws: a scale out of range")
        with np.errstate(all="ignore"):
            w = np.abs(decode(pk(d["wc"][r], d["ws"][r]))).astype(np.float64).reshape(128, 512, 4)
            if not np.max(np.sum(w, axis=(0, 2))) <= 1024: b.append("W: the sizes of a column add up to more than 1024")
    return b
def moves(s, p, ln):
    at = C * np.arange(8)[:, None] + p
    has = at.copy()
    for i in range(STEPS):
        link = 2 * ln[T * i:T * i + T] + (s[16 * i + 1] > 0)
        push, stack, own = s[16 * i] > 0, has[:, :T].copy(), has[link % 8, T + link // 8]
        has[:, :T] = np.where(push, np.concatenate([own[None], stack[:7]]), np.concatenate([stack[1:], own[None]]))
        has[link % 8, T + link // 8] = np.where(push, stack[7], stack[0])
    m = np.zeros(8 * C, np.int64)
    m[at] = has
    return m
def moved(t, m):
    z = t.reshape(8, 16, C, 4).transpose(0, 2, 1, 3).reshape(8 * C, 16, 4)[m]
    return np.ascontiguousarray(z.reshape(8, C, 16, 4).transpose(0, 2, 1, 3)).reshape(128, 4 * C)
def reference(x, u, v, p, ln, wc, ws):
    qu = [mx_ref.quantize(u[r]) for r in range(N)]
    lay = [pk(wc[r], ws[r]) for r in range(N)]
    now = [x[r] for r in range(N)]
    for a in MATES:
        m, qz = [], []
        for r in range(N):
            s = mx_ref.matmul(qu[r], mx_ref.quantize(np.ascontiguousarray(now[r][:, :4 * T])))
            m.append(moves(s, gentries(p[r]), entries(ln[r])))
            qz.append(mx_ref.quantize(moved(now[r], m[r])))
        for r in range(N):
            h = join(pick(qz[r ^ a], np.arange(K)), pick(qz[r], np.arange(K, C)))
            has = decode(h)
            made = tile([np.maximum(mx_ref.matmul(pick(lay[r], np.arange(128 * b, 128 * b + 128)), h), np.float32(0.0)) * np.float32(0.015625) + has[:, b::4] for b in range(4)])
            now[r] = moved(made, np.argsort(m[r]))
    y, op = np.zeros((N, 128, C), np.float32), np.zeros((N, 8, C), np.float32)
    oc, osc = np.zeros((N, 128, 4 * C), np.uint8), np.zeros((N, 16, C), np.uint8)
    for r in range(N):
        q = mx_ref.quantize(now[r])
        y[r] = mx_ref.matmul(mx_ref.quantize(v[r]), q)
        op[r] = m[r].reshape(8, C)
        oc[r], osc[r] = emit(q)
    return {"y": y, "op": op, "oc": oc, "osc": osc}

@@ -1,0 +1,638 @@
+from concourse.mybir import dt, AluOpType, ActivationFunctionType
+
+C, ST, KX, STEPS, N = 400, 320, 96, 3, 8
+MATES = [1, 2, 4]
+W8 = 8 * 4 * C
+OP = AluOpType
+COPY, RELU = ActivationFunctionType.Copy, ActivationFunctionType.Relu
+CODES = "float8_e4m3fn_x4"
+
+SCRATCH = {
+    "R": ("sbuf", [128, W8], "bfloat16"), "XT": ("sbuf", [128, 4 * C], "bfloat16"), "ZT": ("sbuf", [128, 4 * C], "bfloat16"),
+    "UT": ("sbuf", [128, 512], "bfloat16"), "VT": ("sbuf", [128, 512], "bfloat16"),
+    "ET": ("sbuf", [128, 2048], "bfloat16"), "ONE": ("sbuf", [128, 512], "bfloat16"),
+    "KWT": ("sbuf", [128, 2048], "bfloat16"), "BT": ("sbuf", [128, 768], "bfloat16"),
+    "LP": ("sbuf", [128, 25], "int32"), "LN": ("sbuf", [128, 60], "int32"),
+    "PU": ("sbuf", [128, 26], "uint16"), "LNU": ("sbuf", [128, 60], "uint16"),
+    "LOF0": ("sbuf", [128, 60], "uint16"), "LOF1": ("sbuf", [128, 60], "uint16"),
+    "LX0": ("sbuf", [128, 60], "uint16"), "LX1": ("sbuf", [128, 60], "uint16"),
+    "CM0": ("sbuf", [128, 26], "uint16"), "CM1": ("sbuf", [128, 26], "uint16"), "LTL": ("sbuf", [128, 6], "uint16"),
+    "UL": ("sbuf", [128, 8], "uint16"), "CLU": ("sbuf", [128, 6], "uint16"),
+    "KU0": ("sbuf", [128, 20], "uint16"), "KU1": ("sbuf", [128, 20], "uint16"),
+    "LU0": ("sbuf", [128, 40], "uint16"), "LU1": ("sbuf", [128, 40], "uint16"),
+    "OFZ": ("sbuf", [128, 104], "uint16"), "OFX": ("sbuf", [128, 104], "uint16"),
+    "IQ": ("sbuf", [128, 960], "bfloat16"), "MASK": ("sbuf", [128, 960], "bfloat16"), "SEG": ("sbuf", [128, 960], "bfloat16"),
+    "IDT": ("sbuf", [128, 512], "float32"), "ID5": ("sbuf", [128, 320], "float32"), "GI": ("sbuf", [128, 64], "bfloat16"),
+    "THR": ("sbuf", [128, 64], "float32"), "IDX": ("sbuf", [128, 128], "int32"), "SC": ("sbuf", [128, 24], "float32"), "KC": ("sbuf", [128, 3], "float32"),
+    "QQ": ("sbuf", [128, 1280], "float32"), "VA": ("sbuf", [128, 640], "float32"), "MF": ("sbuf", [128, 400], "float32"), "ML": ("sbuf", [128, 240], "float32"),
+    "CF": ("sbuf", [128, 400], "float32"), "MG": ("sbuf", [128, 960], "float32"), "SN": ("sbuf", [128, 960], "float32"),
+    "KF0": ("sbuf", [128, 320], "bfloat16"), "KF1": ("sbuf", [128, 320], "bfloat16"),
+    "MK": ("sbuf", [128, 960], "bfloat16"), "SCK": ("sbuf", [128, 960], "bfloat16"),
+    "DF0": ("sbuf", [128, 2048], "float32"), "DF1": ("sbuf", [128, 2048], "float32"),
+    "DI0": ("sbuf", [128, 640], "int32"), "DI1": ("sbuf", [128, 640], "int32"),
+    "T0": ("sbuf", [128, 8 * C], "float32"), "TN": ("sbuf", [128, 8 * C], "float32"),
+    "FL0": ("sbuf", [128, 640], "float32"), "FL1": ("sbuf", [128, 640], "float32"), "FLO": ("sbuf", [128, 640], "float32"),
+    "OPF": ("sbuf", [128, 400], "float32"), "RL": ("sbuf", [128, 1216], "float32"), "RL2": ("sbuf", [128, 512], "float32"), "YO": ("sbuf", [128, 400], "float32"),
+    "PS": ("psum", [128, 4096], "float32"),
+}
+for _n, _w in (("U", 128), ("UP", 128), ("V", 128), ("W", 512), ("E", 512), ("K", 512), ("B", 192), ("X", C), ("S", 128), ("R", KX)):
+    SCRATCH["Q" + _n] = ("sbuf", [128, _w], CODES)
+    SCRATCH["S" + _n] = ("sbuf", [128, _w], "uint8")
+for _r in range(STEPS):
+    SCRATCH["HQ%d" % _r] = ("sbuf", [128, C], CODES)
+    SCRATCH["HS%d" % _r] = ("sbuf", [128, C], "uint8")
+DMAS = ["d_ln", "d_p", "d_u", "d_x", "d_xs", "d_v", "d_w", "d_t0", "d_tn0", "d_tn1", "d_out", "d_op"]
+DMAS += ["d_%s%d" % (k, r) for k in ("ye", "yl") for r in range(STEPS)]
+SEMAPHORES = ["ev", "es", "et", "eg", "rarr", "rsent"] + DMAS + ["arr%d" % r for r in range(STEPS)] + ["snt%d" % r for r in range(STEPS)]
+
+
+def hops(T, topo, i, r):
+    src, dst = T.cores[i], T.cores[i ^ MATES[r]]
+    if topo.may_write(src, dst):
+        return None, None
+    c = [k for k in topo.cores_of(src) if k not in T.cores and topo.die(k) == topo.die(src) and topo.may_write(k, dst)]
+    return c[0], c[-1]
+
+
+def mask_of(topo, src, dst):
+    e = topo.engines(src, dst)[:8]
+    return sum(1 << k for k in e), len(e)
+
+
+def relay(g, core, T, topo):
+    for i in range(N):
+        for r in range(STEPS):
+            pair = hops(T, topo, i, r)
+            if core not in pair:
+                continue
+            src, dst = T.cores[i], T.cores[i ^ MATES[r]]
+            jobs = [k for k in range(2) if pair[k] == core]
+            n_in = mask_of(topo, src, core)[1]
+            m, n = mask_of(topo, core, dst)
+            rid, pid = topo.addr(dst, core)
+            g.wait_ge(T.sem.rarr, n_in * len(jobs))
+            for k in jobs:
+                if k == 0:
+                    o, s = T["HQ%d" % r][:, 0:KX].bitcast(dt.uint8), T.QR[:, 0:KX].bitcast(dt.uint8)
+                else:
+                    o, s = T["HS%d" % r][:, 0:KX], T.SR[:, 0:KX]
+                g.remote_dma(out_ap=o, in_ap=s, remote_sem=T.sem["arr%d" % r], local_sem=T.sem.rsent, pid=pid, routing_id=rid, dma_engine_mask=m)
+            g.wait_ge(T.sem.rsent, n * len(jobs))
+
+
+def A(name, a, b, s=1):
+    return ("A", name, a, b, s)
+
+
+def IND(win, off):
+    return ("I", win, off)
+
+
+def CW(name, a, b):
+    return ("C", name, a, b, 1)
+
+
+def is_ap(x):
+    return isinstance(x, tuple) and len(x) > 0 and x[0] in ("A", "I", "C")
+
+
+def builder(g, T):
+    Q = {"v": g.vector, "s": g.scalar, "t": g.tensor, "g": g, "y": g.sync}
+    known = {q: {} for q in Q}
+    total, clock, hist, waited, pending = {}, {}, {}, {}, {}
+
+    def ap(x):
+        if x[0] == "A":
+            _, n, a, b, s = x
+            return T[n][:, a:b] if s == 1 else T[n][:, a:b:s]
+        if x[0] == "C":
+            return T[x[1]][:, x[2]:x[3]].bitcast(dt.uint32)
+        return ap(x[1]).indirect(ap(x[2]))
+
+    def region(x):
+        _, n, a, b, s = x
+        if n == "PS":
+            return n, (a // 512 * 512, (b + 511) // 512 * 512, 1)
+        return n, (a, b, s)
+
+    def meet(p, q):
+        if p[1] <= q[0] or q[1] <= p[0]:
+            return False
+        return not (p[2] == q[2] > 1 and (p[0] - q[0]) % p[2])
+
+    def wait(q, evs):
+        best = {}
+        for s, v in set(evs):
+            if known[q].get(s, 0) < v:
+                best[s] = max(v, best.get(s, 0))
+        evs = [e for e in best.items() if not any(o != e[0] and clock[(o, w)].get(e[0], 0) >= e[1] for o, w in best.items())]
+        for s, v in sorted(evs):
+            Q[q].wait_ge(T.sem[s], v)
+            waited[s] = max(v, waited.get(s, 0))
+            for k, w in clock[(s, v)].items():
+                known[q][k] = max(w, known[q].get(k, 0))
+
+    def hazards(q, reads, writes, acc=False):
+        evs = []
+        for x, w in [(r, False) for r in reads] + [(r, True) for r in writes]:
+            n, reg = region(x)
+            for reg2, w2, ev, q2 in hist.get(n, []):
+                if meet(reg, reg2) and (w or w2 or (n == "PS" and q2 != q)) and not (acc and q2 == q):
+                    evs.append(ev)
+        wait(q, evs)
+
+    def note(q, reads, writes, ev):
+        for x, w in [(r, False) for r in reads] + [(r, True) for r in writes]:
+            n, reg = region(x)
+            h = hist.setdefault(n, [])
+            if w and reg[2] == 1:
+                h[:] = [e for e in h if not (reg[0] <= e[0][0] and e[0][1] <= reg[1])]
+            h[:] = [e for e in h if not (e[0] == reg and e[1] == w and e[3] == q and e[2][0] == ev[0])]
+            h.append((reg, w, ev, q))
+
+    def parts(xs):
+        out = []
+        for x in xs:
+            if is_ap(x):
+                out += [("A",) + x[1][1:], x[2]] if x[0] == "I" else [("A",) + x[1:]]
+        return out
+
+    def emit(q, fn, nout, *args, acc=False, **kw):
+        writes, reads = [], parts(args[nout:]) + parts(kw.values())
+        for x in args[:nout]:
+            if x[0] == "I":
+                writes.append(("A",) + x[1][1:])
+                reads.append(x[2])
+            else:
+                writes.append(("A",) + x[1:])
+        hazards(q, reads, writes, acc)
+        s = "e" + q
+        i = fn(*[ap(x) if is_ap(x) else x for x in args], **{k: ap(x) if is_ap(x) else x for k, x in kw.items()})
+        i.then_inc(T.sem[s], 1)
+        total[s] = total.get(s, 0) + 1
+        c = dict(known[q])
+        c[s] = total[s]
+        clock[(s, total[s])] = c
+        note(q, reads, writes, (s, total[s]))
+
+    def batch(sem, q, reads, writes):
+        o = pending.setdefault(sem, [[], [], {}])
+        o[0] += list(reads)
+        o[1] += list(writes)
+        for k, v in known[q].items():
+            o[2][k] = max(v, o[2].get(k, 0))
+
+    def dma(q, sem, out, in_, reads=(), writes=()):
+        hazards(q, reads, writes)
+        Q[q].dma_start(out, in_).then_inc(T.sem[sem], 16)
+        total[sem] = total.get(sem, 0) + 16
+        batch(sem, q, reads, writes)
+
+    def close(sem):
+        reads, writes, c = pending.pop(sem)
+        c[sem] = total[sem]
+        clock[(sem, total[sem])] = c
+        note("dma", reads, writes, (sem, total[sem]))
+
+    def remote(out, in_, reads, rsem, lsem, addr, m, n):
+        hazards("g", reads, [])
+        g.remote_dma(out_ap=out, in_ap=in_, remote_sem=T.sem[rsem], local_sem=T.sem[lsem], pid=addr[1], routing_id=addr[0], dma_engine_mask=m)
+        total[lsem] = total.get(lsem, 0) + n
+        batch(lsem, "g", reads, [])
+
+    def arrives(writes, sem, n):
+        total[sem] = n
+        clock[(sem, n)] = {sem: n}
+        note("remote", [], writes, (sem, n))
+
+    def finish():
+        for s in sorted(total):
+            if waited.get(s, 0) < total[s]:
+                g.wait_ge(T.sem[s], total[s])
+
+    return emit, dma, close, remote, arrives, finish
+
+
+def rank_program(g, core, T, topo):
+    rank = T.rank_of(core)
+    if rank is None:
+        relay(g, core, T, topo)
+        return
+    emit, dma, close, remote, arrives, finish = builder(g, T)
+    V, S = g.vector, g.scalar
+
+    def ts(out, x, s1, op0, s2=None, op1=None):
+        if op1 is None:
+            emit("v", V.tensor_scalar, 1, out, x, s1, None, op0)
+        else:
+            emit("v", V.tensor_scalar, 1, out, x, s1, s2, op0, op1)
+
+    def tt(out, x, y, op):
+        emit("v", V.tensor_tensor, 1, out, x, y, op)
+
+    def cp(out, x):
+        emit("v", V.tensor_copy, 1, out, x)
+
+    def act(out, x, func=COPY, **kw):
+        emit("s", S.activation, 1, out, x, func, **kw)
+
+    def quant(n, a, b, x, sn=None):
+        emit("v", V.quantize_mx, 2, A(n, a, b), A(sn or "S" + n[1:], a, b), x)
+
+    def mm(out, l, ls, r, rs, start=True, stop=True):
+        emit("t", g.tensor.matmul_mx, 1, out, l, ls, r, rs, start, stop, acc=not start)
+
+    def iota(out, pattern, base, cm, whole=False):
+        if whole:
+            emit("g", g.iota, 1, out, pattern, base, cm)
+        else:
+            emit("g", g.iota, 1, out, pattern, base, cm, allow_small_or_imprecise_dtypes=True)
+
+    def sc(i):
+        return A("SC", i, i + 1)
+
+    def ix(a, b):
+        return A("IDX", a, b)
+
+    def shifted(sem, queues, name, width, src, a, b, reads):
+        n = 0
+        for k in range(1, 8):
+            for d0, s0, rows in ((0, 16 * k, 128 - 16 * k), (128 - 16 * k, 0, 16 * k)):
+                dma(queues[n % len(queues)], sem, T[name][d0:d0 + rows, width * k + a:width * k + b], src[s0:s0 + rows, a:b],
+                    reads=reads, writes=[A(name, width * k + a, width * k + b)])
+                n += 1
+        close(sem)
+
+    for k in range(8):
+        dma("y", "d_ln", T.LN[16 * k:16 * k + 16, :], T.ln[:, :], writes=[A("LN", 0, 60)] if k == 7 else [])
+    close("d_ln")
+    dma("s", "d_p", T.LP[:, :], T.p[:, :], writes=[A("LP", 0, 25)])
+    close("d_p")
+    dma("s", "d_u", T.UT[:, :], T.u[:, :], writes=[A("UT", 0, 512)])
+    close("d_u")
+    dma("y", "d_x", T.R[:, 0:4 * C], T.x[:, :], writes=[A("R", 0, 4 * C)])
+    close("d_x")
+    dma("y", "d_w", T.QW[:, :].bitcast(dt.uint8), T.wc[:, :], writes=[A("QW", 0, 512)])
+    dma("y", "d_w", T.SW[:, :], T.ws[:, :], writes=[A("SW", 0, 512)])
+    close("d_w")
+    dma("y", "d_v", T.VT[:, :], T.v[:, :], writes=[A("VT", 0, 512)])
+    close("d_v")
+
+    iota(ix(0, 1), [[0, 1]], 0, 1, True)
+    iota(A("GI", 0, 64), [[0, 2], [1, 8], [0, 4]], 0, 0)
+    iota(ix(16, 36), [[16, 20]], 0, 0, True)
+    iota(ix(36, 41), [[64, 5]], 0, 0, True)
+    iota(ix(48, 56), [[0, 8]], 0, 0, True)
+    iota(A("IDT", 0, 512), [[1, 512]], 0, 0)
+    iota(A("ID5", 0, 320), [[512, 320]], 0, 0)
+    iota(A("IQ", 0, 960), [[0, 60], [1, 16]], 0, 0)
+    for i, k in enumerate((3.0, -1.0, 1.0)):
+        emit("v", V.memset, 1, A("KC", i, i + 1), k)
+    emit("v", V.memset, 1, A("ONE", 0, 512), 1.0)
+    emit("v", V.memset, 1, A("BT", 0, 768), 0.0)
+    for i, seq in enumerate((((16, -1), (32, 7), (48, -1), (80, 0), (96, -1), (112, 4)), ((16, 2), (32, -1), (96, 0), (112, -1)), ((16, -1), (112, 0)))):
+        for p0, k in seq:
+            emit("g", g.affine_select, 1, A("KC", i, i + 1), A("KC", i, i + 1), [[0, 1]], OP.is_gt, float(k), p0, -1)
+    for b in range(4):
+        emit("g", g.affine_select, 1, A("ET", 512 * b, 512 * b + 512), A("ONE", 0, 512), [[-1, 512]], OP.is_equal, 0.0, b, 4)
+
+    ts(ix(1, 2), ix(0, 1), 15, OP.bitwise_and)
+    ts(ix(2, 3), ix(0, 1), 4, OP.logical_shift_right)
+    ts(ix(3, 4), ix(0, 1), 5, OP.logical_shift_right)
+    ts(ix(4, 5), ix(0, 1), 3, OP.bitwise_and)
+    ts(ix(5, 6), ix(0, 1), 4, OP.logical_shift_right, 1, OP.bitwise_and)
+    cp(sc(0), ix(1, 2))
+    cp(sc(1), ix(2, 3))
+    ts(sc(2), ix(2, 3), 400, OP.mult)
+    cp(sc(3), ix(5, 6))
+    ts(sc(4), ix(5, 6), 400, OP.mult)
+    cp(sc(9), ix(3, 4))
+    ts(sc(5), ix(4, 5), 3, OP.is_equal, -47, OP.mult)
+    ts(sc(6), ix(4, 5), 16, OP.mult)
+    tt(sc(7), sc(6), sc(5), OP.add)
+    ts(sc(8), sc(6), 17, OP.add)
+    ts(sc(10), sc(0), 4, OP.mult)
+    tt(sc(11), sc(10), sc(9), OP.add)
+
+    cp(A("PU", 0, 25), A("LP", 0, 25))
+    act(A("T0", 0, C), IND(A("IDT", 0, 512), A("PU", 0, 25)), ActivationFunctionType.Identity, bias=sc(2))
+    shifted("d_t0", "y", "T0", C, T.T0, 0, C, [A("T0", 0, C)])
+    shifted("d_xs", "y", "R", 4 * C, T.x, 0, 4 * C, [])
+
+    cp(A("LNU", 0, 60), A("LN", 0, 60))
+    emit("v", V.tensor_copy, 1, IND(A("QQ", 0, 320), A("LNU", 0, 20)), A("IDT", 0, 320))
+    tt(A("VA", 0, 320), IND(A("ID5", 0, 320), A("LNU", 0, 20)), A("IDT", 0, 320), OP.add)
+    cp(A("LOF0", 0, 40), A("LN", 20, 60))
+    ts(A("LOF0", 40, 60), A("LN", 40, 60), 320, OP.add)
+    emit("v", V.tensor_copy, 1, IND(A("QQ", 320, 640), A("LNU", 20, 40)), A("VA", 0, 320))
+    ts(A("MASK", 0, 960), A("IQ", 0, 960), sc(0), OP.is_equal)
+    act(A("SEG", 0, 960), A("IQ", 0, 960), ActivationFunctionType.Sign)
+    ts(A("THR", 0, 64), A("GI", 0, 64), sc(1), OP.not_equal, 1.0e29, OP.mult)
+    ts(A("UL", 0, 8), ix(48, 56), sc(7), OP.add)
+    ts(A("UL", 2, 4), ix(48, 50), sc(8), OP.add)
+    ts(A("CLU", 0, 5), ix(36, 41), sc(11), OP.add)
+    for i, ws in enumerate(((1, 2, 4, 8), (16, 32, 0, 0), (-4, -2, -1, 32), (16, 8, 0, 0))):
+        for t in range(4):
+            act(A("KWT", 512 * i + t, 512 * i + 512, 4), A("MASK", 0, 128), scale=float(ws[t]))
+
+    def spread(out, in_, n):
+        emit("v", V.tensor_tensor_scan, 1, out, A("SEG", 0, n), in_, 0.0, OP.mult, OP.add)
+
+    off = {}
+    for buf, pairs in (
+        ("DF", [("ST", 80), ("BASE", 60), ("JS", 20), ("JR", 20), ("VV", 80), ("E", 40), ("OR0", 20), ("OR1", 40), ("f0", 20), ("f1", 40), ("fB", 40),
+                ("s12", 20), ("cnt", 20), ("t1", 20), ("t2", 20), ("t3", 20), ("t4", 20), ("t5", 60), ("n2", 20), ("nb", 20), ("t6", 20), ("t7", 20), ("t8", 40),
+                ("X", 20), ("ZZ", 40), ("m1", 20), ("t9", 20), ("ta", 20), ("v1", 40), ("ne", 20), ("tb", 20), ("oe", 20), ("tc", 20), ("on", 20),
+                ("td", 20), ("te", 20), ("o1", 40), ("mz", 40), ("tf", 40), ("tg", 40), ("w", 40), ("my", 40), ("th", 40), ("ti", 40), ("v2", 40),
+                ("u1", 40), ("u2", 40), ("u3", 40), ("u4", 40), ("u5", 40), ("RES", 40), ("u6", 40), ("RS2", 40), ("q1", 80), ("q2", 60), ("q3", 60), ("q4", 60)]),
+        ("DI", [("P", 120), ("k7", 20), ("KG", 60), ("gb", 60), ("c0x", 20), ("c0y", 20), ("c0z", 40), ("c1y", 40), ("yb1", 20), ("KO", 20),
+                ("a1", 60), ("a2", 60), ("pk", 20), ("pa", 20), ("pr", 20), ("pb", 20)])):
+        at = 0
+        for n, w in pairs:
+            off[n] = (buf, at, w)
+            at += w
+
+    def d_(d, n, a=0, b=None):
+        buf, at, w = off[n]
+        return A("%s%d" % (buf, d), at + a, at + (w if b is None else b))
+
+    def statics(d):
+        D = lambda n, a=0, b=None: d_(d, n, a, b)
+        tt(A("MG", 0, 960), IND(A("QQ", 0, 640 if d == 0 else 1280), A("LOF%d" % d, 0, 60)), A("MASK", 0, 960), OP.mult)
+        spread(A("SN", 0, 960), A("MG", 0, 960), 960)
+        cp(D("pk"), A("SN", 655, 960, 16))
+        cp(A("LX%d" % d, 0, 40), A("SN", 15, 640, 16))
+        ts(D("ST", 0, 40), A("SN", 15, 640, 16), sc(2), OP.subtract)
+        ts(D("pa"), D("pk"), 511, OP.bitwise_and)
+        ts(D("pr"), D("pk"), 9, OP.logical_shift_right, 3, OP.bitwise_and)
+        ts(D("pb"), D("pk"), 11, OP.logical_shift_right)
+        cp(A("LX%d" % d, 40, 60), D("pa"))
+        ts(D("ST", 40, 60), D("pa"), sc(2), OP.subtract, 400, OP.add)
+        ts(D("q3", 0, 20), D("pr"), 800, OP.mult, 320, OP.add)
+        ts(D("q4", 0, 20), D("pb"), sc(2), OP.subtract)
+        tt(D("ST", 60, 80), D("q3", 0, 20), D("q4", 0, 20), OP.add)
+        ts(D("q1"), D("ST"), 0.0, OP.is_lt, 3200, OP.mult)
+        tt(D("ST"), D("ST"), D("q1"), OP.add)
+        if d == 0:
+            ts(D("a1"), A("LN", 0, 60), 3, OP.bitwise_and)
+            ts(D("a2"), A("LN", 0, 60), 2, OP.logical_shift_right)
+            ts(D("q3"), D("a1"), 800, OP.mult, 320, OP.add)
+            ts(D("q4"), D("a2"), sc(2), OP.subtract)
+            tt(D("BASE"), D("q3"), D("q4"), OP.add)
+            ts(D("q2"), D("BASE"), 0.0, OP.is_lt, 3200, OP.mult)
+            tt(D("BASE"), D("BASE"), D("q2"), OP.add)
+        else:
+            for i in range(3):
+                cp(D("BASE", 20 * i, 20 * i + 20), d_(0, "BASE", 40 - 20 * i, 60 - 20 * i))
+        ts(D("VV", 60, 80), D("BASE", 40, 60), sc(4), OP.add)
+        ts(D("E", 20, 40), ix(16, 36), 0.0, OP.mult, sc(3), OP.add)
+        ts(D("t1"), ix(16, 36), sc(0), OP.add)
+        ts(D("JS"), D("t1"), 4400, OP.add)
+        ts(D("t2"), D("t1"), sc(2), OP.subtract)
+        ts(D("t3"), D("t2"), 0.0, OP.is_lt, 3200, OP.mult)
+        ts(D("t4"), D("t2"), 800, OP.add)
+        tt(D("JR"), D("t3"), D("t4"), OP.add)
+
+    def early(d):
+        D = lambda n, a=0, b=None: d_(d, n, a, b)
+        P = lambda r, k=1: d_(d, "P", 20 * r, 20 * r + 20 * k)
+        ops = [lambda r=r: ts(P(r), D("KO"), r, OP.logical_shift_right, 1, OP.bitwise_and) for r in range(6)]
+        return ops + [
+            lambda: ts(D("k7"), D("KO"), 7, OP.bitwise_and),
+            lambda: tt(D("s12"), P(1), P(2), OP.add),
+            lambda: ts(D("t5"), P(3, 3), 400, OP.mult),
+            lambda: ts(D("t2"), P(1), 2000, OP.mult),
+            lambda: ts(D("t3"), P(0), -800, OP.mult),
+            lambda: ts(D("n2"), P(5), sc(3), OP.is_equal),
+            lambda: cp(D("E", 0, 20), P(5)),
+            lambda: ts(D("fB", 0, 20), P(2), A("KC", 2, 3), OP.is_equal),
+            lambda: tt(D("cnt"), D("s12"), P(0), OP.add),
+            lambda: tt(D("VV", 0, 60), D("t5"), D("BASE"), OP.add),
+            lambda: ts(D("f0"), D("k7"), A("KC", 0, 1), OP.is_equal),
+            lambda: ts(D("f1", 0, 20), D("s12"), A("KC", 1, 2), OP.is_equal),
+            lambda: ts(D("nb"), D("s12"), 1.0, OP.is_equal),
+            lambda: tt(D("t4"), D("t2"), D("t3"), OP.add),
+            lambda: ts(D("t1"), D("cnt"), -800, OP.mult),
+            lambda: ts(D("fB", 20, 40), D("n2"), -1.0, OP.mult, 1.0, OP.add),
+            lambda: tt(D("f1", 20, 40), D("n2"), D("nb"), OP.mult),
+            lambda: tt(D("OR1", 20, 40), D("t4"), D("JR"), OP.add),
+            lambda: tt(D("OR0"), D("t1"), D("JS"), OP.add),
+            lambda: tt(D("t6"), D("VV", 0, 20), D("OR0"), OP.subtract),
+            lambda: tt(D("t7"), D("t6"), D("f0"), OP.mult),
+            lambda: tt(D("OR1", 0, 20), D("t7"), D("OR0"), OP.add),
+        ]
+
+    def gather_k(d):
+        tt(A("MK", 0, 960), IND(A("KF%d" % d, 0, 320), A("LX%d" % d, 0, 60)), A("MASK", 0, 960), OP.mult)
+
+    def late(d):
+        D = lambda n, a=0, b=None: d_(d, n, a, b)
+        V1, x, z, y = D("VV", 20, 40), D("KG", 0, 20), D("KG", 20, 40), D("KG", 40, 60)
+        sh, an = OP.logical_shift_right, OP.bitwise_and
+        spread(A("SCK", 0, 960), A("MK", 0, 960), 960)
+        cp(D("KG"), A("SCK", 15, 960, 16))
+        ts(D("c0x"), x, 3, sh, 1, an)
+        ts(D("gb"), D("KG"), 1, an)
+        ts(D("yb1"), y, 1, sh, 1, an)
+        ts(D("c0y"), y, 3, sh, 1, an)
+        for h in (0, 20):
+            ts(D("c0z", h, h + 20), z, 3, sh, 1, an)
+            ts(D("c1y", h, h + 20), y, 4, sh, 1, an)
+        tt(D("m1"), D("c0x"), D("P", 80, 100), OP.is_equal)
+        ts(D("t8"), D("gb", 0, 40), 2800, OP.mult)
+        tt(D("ne"), D("gb", 40, 60), D("yb1"), OP.not_equal)
+        ts(D("tb"), D("gb", 40, 60), 2000, OP.mult)
+        ts(D("tc"), D("c0y"), 400, OP.mult)
+        tt(D("mz"), D("c0z"), D("E"), OP.is_equal)
+        tt(D("my"), D("c1y"), D("E"), OP.is_equal)
+        tt(D("X"), D("t8", 0, 20), D("ST", 0, 20), OP.add)
+        for h in (0, 20):
+            tt(D("ZZ", h, h + 20), D("t8", 20, 40), D("ST", 20, 40), OP.add)
+        tt(D("oe"), D("tb"), D("ST", 40, 60), OP.add)
+        tt(D("on"), D("tc"), D("ST", 60, 80), OP.add)
+        tt(D("t9"), D("X"), V1, OP.subtract)
+        tt(D("tf"), D("ZZ"), D("VV", 40, 80), OP.subtract)
+        tt(D("td"), D("on"), D("oe"), OP.subtract)
+        tt(D("ta"), D("t9"), D("m1"), OP.mult)
+        tt(D("tg"), D("tf"), D("mz"), OP.mult)
+        tt(D("te"), D("td"), D("ne"), OP.mult)
+        for h in (0, 20):
+            tt(D("v1", h, h + 20), D("ta"), V1, OP.add)
+        tt(D("w"), D("tg"), D("VV", 40, 80), OP.add)
+        for h in (0, 20):
+            tt(D("o1", h, h + 20), D("te"), D("oe"), OP.add)
+        tt(D("u1"), D("v1"), D("OR1"), OP.subtract)
+        tt(D("th"), D("o1"), D("w"), OP.subtract)
+        tt(D("u2"), D("u1"), D("f1"), OP.mult)
+        tt(D("ti"), D("th"), D("my"), OP.mult)
+        tt(D("u3"), D("u2"), D("OR1"), OP.add)
+        tt(D("v2"), D("ti"), D("w"), OP.add)
+        tt(D("u4"), D("v2"), D("OR1"), OP.subtract)
+        tt(D("u5"), D("u4"), D("fB"), OP.mult)
+        tt(D("RES"), D("u3"), D("u5"), OP.add)
+        ts(D("u6"), D("RES"), 3200, OP.is_ge, -3200, OP.mult)
+        tt(D("RS2"), D("RES"), D("u6"), OP.add)
+        cp(A("LU%d" % d, 0, 40), D("RS2"))
+
+    def lookup(d, table, out, scalar_only=False):
+        a = (A(out, 0, 320), IND(A(table, 0, 8 * C), A("LU%d" % d, 0, 20)))
+        if scalar_only:
+            act(*a)
+        else:
+            cp(*a)
+        act(A(out, 320, 640), IND(A(table, 0, 8 * C), A("LU%d" % d, 20, 40)))
+
+    def offsets(out, d, flat, cm, cols):
+        n = cols // 16
+        tt(A("MG", 0, cols), IND(A(flat, 0, 640), A(cm, 0, n)), A("MASK", 0, cols), OP.mult)
+        spread(A("SN", 0, cols), A("MG", 0, cols), cols)
+        ts(d_(d, "u1", 0, n), A("SN", 15, cols, 16), sc(2), OP.subtract)
+        ts(d_(d, "u2", 0, n), d_(d, "u1", 0, n), 0.0, OP.is_lt, 3200, OP.mult)
+        tt(d_(d, "u3", 0, n), d_(d, "u1", 0, n), d_(d, "u2", 0, n), OP.add)
+        for t in (2, 3, 0, 1):
+            ts(A(out, 26 * t, 26 * t + n), d_(d, "u3", 0, n), 4, OP.mult, t, OP.add)
+
+    def pull(dst, offs, c0, c1):
+        for t in (2, 0, 3, 1):
+            a = (A(dst, 4 * c0 + t, 4 * c1, 4), IND(A("R", 0, W8), A(offs, 26 * t + c0 // 16, 26 * t + c1 // 16)))
+            if t >= 2:
+                act(*a)
+            else:
+                cp(*a)
+
+    def scores(src):
+        quant("QX", 0, ST, A(src, 0, 4 * ST))
+        for n, c0 in enumerate((0, 128, 192)):
+            mm(A("PS", 512 * n, 512 * n + 128), A("QX", c0, c0 + 128), A("SX", c0, c0 + 128), A("QUP", 0, 128), A("SUP", 0, 128))
+        for n in range(3):
+            h = 16 if n == 2 else 0
+            for s in (0, 32):
+                o = 8 * s + 32 * n
+                tt(A("BT", o, o + 32 - h), A("PS", 512 * n + s + h, 512 * n + s + 32), A("THR", s + h, s + 32), OP.is_gt)
+        quant("QB", 0, 192, A("BT", 0, 768))
+        for d in range(2):
+            for i in range(2):
+                k = 256 * d + 128 * i
+                mm(A("PS", 1536 + 512 * d, 1664 + 512 * d), A("QK", k, k + 128), A("SK", k, k + 128), A("QB", 64 * i, 64 * i + 128), A("SB", 64 * i, 64 * i + 128), i == 0, i == 1)
+        cp(A("KU0", 0, 20), A("PS", 1536, 1556))
+        cp(d_(0, "KO"), A("PS", 1536, 1556))
+        act(A("KF0", 0, 320), IND(A("IDT", 0, 512), A("KU0", 0, 20)))
+        ts(A("KU1", 0, 20), A("PS", 2048, 2068), 7.0, OP.add)
+        ts(d_(1, "KO"), A("PS", 2048, 2068), 7.0, OP.add)
+
+    quant("QU", 0, 128, A("UT", 0, 512))
+    emit("v", V.tensor_copy, 1, CW("QUP", 0, 128), IND(CW("QU", 0, 128), A("UL", 0, 8)))
+    act(A("SUP", 0, 128), IND(A("SU", 0, 128), A("UL", 0, 8)))
+    quant("QK", 0, 512, A("KWT", 0, 2048))
+    statics(0)
+    emit("v", V.tensor_copy, 1, IND(A("QQ", 640, 960), A("LNU", 40, 60)), A("IDT", 0, 320))
+    scores("R")
+    act(A("MF", 0, 320), A("IDT", 0, 320), scale=1025.0)
+    ts(A("ML", 0, 80), IND(A("QQ", 640, 960), A("CLU", 0, 5)), 320.0, OP.add)
+    ts(A("ML", 80, 160), IND(A("QQ", 0, 320), A("CLU", 0, 5)), 320.0, OP.add)
+    ts(A("ML", 160, 240), A("ML", 80, 160), 1024.0, OP.mult)
+    tt(A("MF", 320, 400), A("ML", 160, 240), A("ML", 0, 80), OP.add)
+    emit("v", V.tensor_copy, 1, IND(A("CF", 0, 400), A("PU", 0, 25)), A("MF", 0, 400))
+    tt(A("MG", 0, 400), A("CF", 0, 400), A("MASK", 0, 400), OP.mult)
+    spread(A("SN", 0, 400), A("MG", 0, 400), 400)
+    cp(ix(64, 89), A("SN", 15, 400, 16))
+    ts(ix(96, 121), ix(64, 89), 1023, OP.bitwise_and)
+    cp(A("CM0", 0, 25), ix(96, 121))
+
+    def statics_back():
+        tt(A("VA", 320, 640), IND(A("ID5", 0, 320), A("LNU", 40, 60)), A("IDT", 0, 320), OP.add)
+        for i, (k, o) in enumerate(((20, 640), (0, 640), (0, 960))):
+            ts(A("LOF1", 20 * i, 20 * i + 20), A("LN", k, k + 20), o, OP.add)
+        emit("v", V.tensor_copy, 1, IND(A("QQ", 960, 1280), A("LNU", 20, 40)), A("VA", 320, 640))
+        statics(1)
+        ts(ix(96, 121), ix(64, 89), 10, OP.logical_shift_right)
+        cp(A("CM1", 0, 25), ix(96, 121))
+        tt(A("MG", 0, 80), A("ML", 80, 160), A("MASK", 0, 80), OP.mult)
+        spread(A("SN", 0, 80), A("MG", 0, 80), 80)
+        cp(A("LTL", 0, 5), A("SN", 15, 80, 16))
+        quant("QV", 0, 128, A("VT", 0, 512))
+
+    quant("QE", 0, 512, A("ET", 0, 2048))
+
+    for r in range(STEPS):
+        HQ, HS = "HQ%d" % r, "HS%d" % r
+        peer = rank ^ MATES[r]
+        n_arr = sum(mask_of(topo, T.cores[peer] if c is None else c, core)[1] for c in hops(T, topo, peer, r))
+        arrives([A(HQ, 0, KX), A(HS, 0, KX)], "arr%d" % r, n_arr)
+        if r:
+            scores("XT")
+        own = early(0)
+        for f in own[:14]:
+            f()
+        gather_k(0)
+        for f in own[14:]:
+            f()
+        late(0)
+        lookup(0, "TN" if r else "T0", "FL0")
+        offsets("OFZ", 0, "FL0", "CM0", C)
+        pull("ZT", "OFZ", 0, 128)
+        quant("QS", 0, 128, A("ZT", 0, 512))
+        for k, c in enumerate(hops(T, topo, rank, r)):
+            to = T.cores[peer] if c is None else c
+            m, n = mask_of(topo, core, to)
+            if k == 0:
+                o = T[HQ if c is None else "QR"][:, 0:KX].bitcast(dt.uint8)
+                i, rd = T.QS[:, 0:KX].bitcast(dt.uint8), [A("QS", 0, KX)]
+            else:
+                o = T[HS if c is None else "SR"][:, 0:KX]
+                i, rd = T.SS[:, 0:KX], [A("SS", 0, KX)]
+            remote(o, i, rd, "arr%d" % r if c is None else "rarr", "snt%d" % r, topo.addr(to, core), m, n)
+        close("snt%d" % r)
+        pull("ZT", "OFZ", 128, C)
+        quant(HQ, KX, C, A("ZT", 4 * KX, 4 * C), HS)
+
+        def layer(c0, c1, m1, buf, w, meanwhile=()):
+            for b in range(4):
+                for n, p in (("W", 0), ("E", 2048)):
+                    mm(A("PS", p + 512 * b, p + 512 * b + m1), A("Q" + n, 128 * b, 128 * b + 128), A("S" + n, 128 * b, 128 * b + 128), A(HQ, c0, c0 + m1), A(HS, c0, c0 + m1))
+            for b in range(4):
+                l = A(buf, w * b, w * b + c1 - c0)
+                act(l, A("PS", 512 * b, 512 * b + c1 - c0), RELU, scale=0.015625)
+                k = 5 if b else 12
+                for f in meanwhile[:k]:
+                    f()
+                meanwhile = meanwhile[k:]
+                tt(A("R", 4 * c0 + b, 4 * c1, 4), l, A("PS", 2048 + 512 * b, 2048 + 512 * b + c1 - c0), OP.add)
+            for f in meanwhile:
+                f()
+
+        act(A("KF1", 0, 320), IND(A("IDT", 0, 512), A("KU1", 0, 20)))
+        layer(KX, C, C - KX, "RL", 304, early(1) if r else [])
+        shifted("d_ye%d" % r, "y", "R", 4 * C, T.R, 4 * KX, 4 * C, [A("R", 4 * KX, 4 * C)])
+        if r == 0:
+            statics_back()
+            for f in early(1):
+                f()
+        gather_k(1)
+        layer(0, KX, 128, "RL2", 128)
+        shifted("d_yl%d" % r, "sy", "R", 4 * C, T.R, 0, 4 * KX, [A("R", 0, 4 * KX)])
+        late(1)
+        lookup(1, "T0", "FL1")
+        cols = ST if r < STEPS - 1 else C
+        offsets("OFX", 1, "FL1", "CM1", cols)
+        if r < STEPS - 1:
+            act(A("TN", 0, ST), A("FL1", 0, ST))
+            act(A("TN", ST, C), IND(A("FL1", 0, 640), A("LTL", 0, 5)))
+            shifted("d_tn%d" % r, "y", "TN", C, T.TN, 0, C, [A("TN", 0, C)])
+        else:
+            lookup(0, "T0", "FLO", True)
+            act(A("OPF", 0, C), IND(A("FLO", 0, 640), A("CM0", 0, 25)))
+            for k in range(8):
+                dma("y", "d_op", T.op[k:k + 1, :], T.OPF[16 * k:16 * k + 1, :], reads=[A("OPF", 0, C)])
+            close("d_op")
+        pull("XT", "OFX", 0, cols)
+
+    quant("QX", 0, C, A("XT", 0, 4 * C))
+    mm(A("PS", 0, C), A("QV", 0, 128), A("SV", 0, 128), A("QX", 0, C), A("SX", 0, C))
+    dma("s", "d_out", T.oc[:, :], T.QX[:, :].bitcast(dt.uint8), reads=[A("QX", 0, C)])
+    for k in range(4):
+        dma("y", "d_out", T.osc[4 * k:4 * k + 4, :], T.SX[32 * k:32 * k + 4, :], reads=[A("SX", 0, C)])
+    cp(A("YO", 0, C), A("PS", 0, C))
+    dma("y", "d_out", T.y[:, :], T.YO[:, :], reads=[A("YO", 0, C)])
+    close("d_out")
+    finish()

@@ -3,6 +3,7 @@ from concourse.mybir import dt, AluOpType, ActivationFunctionType
 C, ST, KX, STEPS, N = 400, 320, 96, 3, 8
 MATES = [1, 2, 4]
 W8 = 8 * 4 * C
+LW = 512
 OP = AluOpType
 COPY, RELU = ActivationFunctionType.Copy, ActivationFunctionType.Relu
 CODES = "float8_e4m3fn_x4"
@@ -23,14 +24,15 @@ SCRATCH = {
     "OFZ": ("sbuf", [128, 104], "uint16"), "OFX": ("sbuf", [128, 104], "uint16"),
     "IQ": ("sbuf", [128, 960], "bfloat16"), "MASK": ("sbuf", [128, 960], "bfloat16"), "SEG": ("sbuf", [128, 960], "bfloat16"),
     "IDT": ("sbuf", [128, 512], "float32"), "ID5": ("sbuf", [128, 320], "float32"), "GI": ("sbuf", [128, 64], "bfloat16"),
-    "THR": ("sbuf", [128, 64], "float32"), "IDX": ("sbuf", [128, 128], "int32"), "SC": ("sbuf", [128, 24], "float32"), "KC": ("sbuf", [128, 3], "float32"),
+    "THR": ("sbuf", [128, 64], "float32"), "IDX": ("sbuf", [128, 128], "int32"), "SC": ("sbuf", [128, 24], "float32"),
+    "SJ": ("sbuf", [128, 60], "float32"), "KC": ("sbuf", [128, 3], "float32"),
     "QQ": ("sbuf", [128, 1280], "float32"), "VA": ("sbuf", [128, 640], "float32"), "MF": ("sbuf", [128, 400], "float32"), "ML": ("sbuf", [128, 240], "float32"),
     "CF": ("sbuf", [128, 400], "float32"), "MG": ("sbuf", [128, 960], "float32"), "SN": ("sbuf", [128, 960], "float32"),
     "KF0": ("sbuf", [128, 320], "bfloat16"), "KF1": ("sbuf", [128, 320], "bfloat16"),
     "MK": ("sbuf", [128, 960], "bfloat16"), "SCK": ("sbuf", [128, 960], "bfloat16"),
     "DF0": ("sbuf", [128, 2048], "float32"), "DF1": ("sbuf", [128, 2048], "float32"),
-    "DI0": ("sbuf", [128, 640], "int32"), "DI1": ("sbuf", [128, 640], "int32"),
-    "T0": ("sbuf", [128, 8 * C], "float32"), "TN": ("sbuf", [128, 8 * C], "float32"),
+    "DI0": ("sbuf", [128, 704], "int32"), "DI1": ("sbuf", [128, 704], "int32"),
+    "T0": ("sbuf", [128, 8 * LW], "float32"), "TN": ("sbuf", [128, 8 * LW], "float32"),
     "FL0": ("sbuf", [128, 640], "float32"), "FL1": ("sbuf", [128, 640], "float32"), "FLO": ("sbuf", [128, 640], "float32"),
     "OPF": ("sbuf", [128, 400], "float32"), "RL": ("sbuf", [128, 1216], "float32"), "RL2": ("sbuf", [128, 512], "float32"), "YO": ("sbuf", [128, 400], "float32"),
     "PS": ("psum", [128, 4096], "float32"),
@@ -254,6 +256,9 @@ def rank_program(g, core, T, topo):
     def ix(a, b):
         return A("IDX", a, b)
 
+    def sj(i):
+        return A("SJ", 20 * i, 20 * i + 20)
+
     def shifted(sem, queues, name, width, src, a, b, reads):
         n = 0
         for k in range(1, 8):
@@ -264,19 +269,14 @@ def rank_program(g, core, T, topo):
         close(sem)
 
     for k in range(8):
-        dma("y", "d_ln", T.LN[16 * k:16 * k + 16, :], T.ln[:, :], writes=[A("LN", 0, 60)] if k == 7 else [])
+        dma("sy"[k % 2], "d_ln", T.LN[16 * k:16 * k + 16, :], T.ln[:, :], writes=[A("LN", 0, 60)])
     close("d_ln")
     dma("s", "d_p", T.LP[:, :], T.p[:, :], writes=[A("LP", 0, 25)])
     close("d_p")
-    dma("s", "d_u", T.UT[:, :], T.u[:, :], writes=[A("UT", 0, 512)])
+    dma("y", "d_u", T.UT[:, :], T.u[:, :], writes=[A("UT", 0, 512)])
     close("d_u")
     dma("y", "d_x", T.R[:, 0:4 * C], T.x[:, :], writes=[A("R", 0, 4 * C)])
     close("d_x")
-    dma("y", "d_w", T.QW[:, :].bitcast(dt.uint8), T.wc[:, :], writes=[A("QW", 0, 512)])
-    dma("y", "d_w", T.SW[:, :], T.ws[:, :], writes=[A("SW", 0, 512)])
-    close("d_w")
-    dma("y", "d_v", T.VT[:, :], T.v[:, :], writes=[A("VT", 0, 512)])
-    close("d_v")
 
     iota(ix(0, 1), [[0, 1]], 0, 1, True)
     iota(A("GI", 0, 64), [[0, 2], [1, 8], [0, 4]], 0, 0)
@@ -286,15 +286,18 @@ def rank_program(g, core, T, topo):
     iota(A("IDT", 0, 512), [[1, 512]], 0, 0)
     iota(A("ID5", 0, 320), [[512, 320]], 0, 0)
     iota(A("IQ", 0, 960), [[0, 60], [1, 16]], 0, 0)
-    for i, k in enumerate((3.0, -1.0, 1.0)):
+    for i, k in enumerate((1536.0, -512.0, 512.0)):
         emit("v", V.memset, 1, A("KC", i, i + 1), k)
-    emit("v", V.memset, 1, A("ONE", 0, 512), 1.0)
-    emit("v", V.memset, 1, A("BT", 0, 768), 0.0)
+    iota(A("ONE", 0, 512), [[0, 512]], 1, 0)
+    iota(A("BT", 0, 768), [[0, 768]], 0, 0)
     for i, seq in enumerate((((16, -1), (32, 7), (48, -1), (80, 0), (96, -1), (112, 4)), ((16, 2), (32, -1), (96, 0), (112, -1)), ((16, -1), (112, 0)))):
         for p0, k in seq:
-            emit("g", g.affine_select, 1, A("KC", i, i + 1), A("KC", i, i + 1), [[0, 1]], OP.is_gt, float(k), p0, -1)
+            emit("g", g.affine_select, 1, A("KC", i, i + 1), A("KC", i, i + 1), [[0, 1]], OP.is_gt, 512.0 * k, p0, -1)
     for b in range(4):
         emit("g", g.affine_select, 1, A("ET", 512 * b, 512 * b + 512), A("ONE", 0, 512), [[-1, 512]], OP.is_equal, 0.0, b, 4)
+    for n in ("T0", "TN"):
+        for k in range(8):
+            iota(A(n, LW * k + C, LW * k + LW), [[0, LW - C]], 0, 0)
 
     ts(ix(1, 2), ix(0, 1), 15, OP.bitwise_and)
     ts(ix(2, 3), ix(0, 1), 4, OP.logical_shift_right)
@@ -304,8 +307,8 @@ def rank_program(g, core, T, topo):
     cp(sc(0), ix(1, 2))
     cp(sc(1), ix(2, 3))
     ts(sc(2), ix(2, 3), 400, OP.mult)
-    cp(sc(3), ix(5, 6))
-    ts(sc(4), ix(5, 6), 400, OP.mult)
+    ts(sc(4), ix(5, 6), LW, OP.mult)
+    ts(sc(12), ix(2, 3), LW, OP.mult, -8192, OP.add)
     cp(sc(9), ix(3, 4))
     ts(sc(5), ix(4, 5), 3, OP.is_equal, -47, OP.mult)
     ts(sc(6), ix(4, 5), 16, OP.mult)
@@ -313,11 +316,19 @@ def rank_program(g, core, T, topo):
     ts(sc(8), sc(6), 17, OP.add)
     ts(sc(10), sc(0), 4, OP.mult)
     tt(sc(11), sc(10), sc(9), OP.add)
+    ts(sj(2), ix(16, 36), sc(0), OP.add)
+    ts(sj(0), sj(2), 9728, OP.add)
+    ts(sj(1), sj(2), sc(12), OP.subtract, 1024, OP.add)
 
     cp(A("PU", 0, 25), A("LP", 0, 25))
     act(A("T0", 0, C), IND(A("IDT", 0, 512), A("PU", 0, 25)), ActivationFunctionType.Identity, bias=sc(2))
-    shifted("d_t0", "y", "T0", C, T.T0, 0, C, [A("T0", 0, C)])
+    shifted("d_t0", "y", "T0", LW, T.T0, 0, C, [A("T0", 0, C)])
     shifted("d_xs", "y", "R", 4 * C, T.x, 0, 4 * C, [])
+    dma("y", "d_w", T.QW[:, :].bitcast(dt.uint8), T.wc[:, :], writes=[A("QW", 0, 512)])
+    dma("y", "d_w", T.SW[:, :], T.ws[:, :], writes=[A("SW", 0, 512)])
+    close("d_w")
+    dma("y", "d_v", T.VT[:, :], T.v[:, :], writes=[A("VT", 0, 512)])
+    close("d_v")
 
     cp(A("LNU", 0, 60), A("LN", 0, 60))
     emit("v", V.tensor_copy, 1, IND(A("QQ", 0, 320), A("LNU", 0, 20)), A("IDT", 0, 320))
@@ -340,13 +351,13 @@ def rank_program(g, core, T, topo):
 
     off = {}
     for buf, pairs in (
-        ("DF", [("ST", 80), ("BASE", 60), ("JS", 20), ("JR", 20), ("VV", 80), ("E", 40), ("OR0", 20), ("OR1", 40), ("f0", 20), ("f1", 40), ("fB", 40),
-                ("s12", 20), ("cnt", 20), ("t1", 20), ("t2", 20), ("t3", 20), ("t4", 20), ("t5", 60), ("n2", 20), ("nb", 20), ("t6", 20), ("t7", 20), ("t8", 40),
-                ("X", 20), ("ZZ", 40), ("m1", 20), ("t9", 20), ("ta", 20), ("v1", 40), ("ne", 20), ("tb", 20), ("oe", 20), ("tc", 20), ("on", 20),
+        ("DF", [("ST", 80), ("BASE", 60), ("VV", 80), ("OR0", 20), ("OR1", 40), ("f0", 20), ("f1", 40), ("fB", 40), ("s12", 20), ("cnt", 20),
+                ("t1", 20), ("t2", 20), ("t3", 20), ("t4", 20), ("n2", 20), ("nb", 20), ("t6", 20), ("t7", 20),
+                ("X", 20), ("ZZ", 40), ("m1", 20), ("t9", 20), ("ta", 20), ("v1", 40), ("ne", 20), ("tb", 20), ("oe", 20), ("on", 20),
                 ("td", 20), ("te", 20), ("o1", 40), ("mz", 40), ("tf", 40), ("tg", 40), ("w", 40), ("my", 40), ("th", 40), ("ti", 40), ("v2", 40),
-                ("u1", 40), ("u2", 40), ("u3", 40), ("u4", 40), ("u5", 40), ("RES", 40), ("u6", 40), ("RS2", 40), ("q1", 80), ("q2", 60), ("q3", 60), ("q4", 60)]),
-        ("DI", [("P", 120), ("k7", 20), ("KG", 60), ("gb", 60), ("c0x", 20), ("c0y", 20), ("c0z", 40), ("c1y", 40), ("yb1", 20), ("KO", 20),
-                ("a1", 60), ("a2", 60), ("pk", 20), ("pa", 20), ("pr", 20), ("pb", 20)])):
+                ("u1", 40), ("u2", 40), ("u3", 40), ("u4", 40), ("u5", 40), ("q3", 60), ("q4", 60)]),
+        ("DI", [("P", 120), ("k7", 20), ("KG", 60), ("gb", 60), ("c0x", 20), ("c0y", 20), ("c0z", 20), ("c1y", 20), ("yb1", 20), ("KO", 20),
+                ("a1", 60), ("a2", 60), ("pk", 20), ("pa", 20), ("pr", 20), ("pb", 20), ("RES", 40), ("RSM", 40)])):
         at = 0
         for n, w in pairs:
             off[n] = (buf, at, w)
@@ -362,61 +373,48 @@ def rank_program(g, core, T, topo):
         spread(A("SN", 0, 960), A("MG", 0, 960), 960)
         cp(D("pk"), A("SN", 655, 960, 16))
         cp(A("LX%d" % d, 0, 40), A("SN", 15, 640, 16))
-        ts(D("ST", 0, 40), A("SN", 15, 640, 16), sc(2), OP.subtract)
+        ts(D("ST", 0, 40), A("SN", 15, 640, 16), sc(12), OP.subtract)
         ts(D("pa"), D("pk"), 511, OP.bitwise_and)
         ts(D("pr"), D("pk"), 9, OP.logical_shift_right, 3, OP.bitwise_and)
         ts(D("pb"), D("pk"), 11, OP.logical_shift_right)
         cp(A("LX%d" % d, 40, 60), D("pa"))
-        ts(D("ST", 40, 60), D("pa"), sc(2), OP.subtract, 400, OP.add)
-        ts(D("q3", 0, 20), D("pr"), 800, OP.mult, 320, OP.add)
-        ts(D("q4", 0, 20), D("pb"), sc(2), OP.subtract)
+        ts(D("ST", 40, 60), D("pa"), sc(12), OP.subtract, LW, OP.add)
+        ts(D("q3", 0, 20), D("pr"), 1024, OP.mult, 320, OP.add)
+        ts(D("q4", 0, 20), D("pb"), sc(12), OP.subtract)
         tt(D("ST", 60, 80), D("q3", 0, 20), D("q4", 0, 20), OP.add)
-        ts(D("q1"), D("ST"), 0.0, OP.is_lt, 3200, OP.mult)
-        tt(D("ST"), D("ST"), D("q1"), OP.add)
         if d == 0:
             ts(D("a1"), A("LN", 0, 60), 3, OP.bitwise_and)
             ts(D("a2"), A("LN", 0, 60), 2, OP.logical_shift_right)
-            ts(D("q3"), D("a1"), 800, OP.mult, 320, OP.add)
-            ts(D("q4"), D("a2"), sc(2), OP.subtract)
+            ts(D("q3"), D("a1"), 1024, OP.mult, 320, OP.add)
+            ts(D("q4"), D("a2"), sc(12), OP.subtract)
             tt(D("BASE"), D("q3"), D("q4"), OP.add)
-            ts(D("q2"), D("BASE"), 0.0, OP.is_lt, 3200, OP.mult)
-            tt(D("BASE"), D("BASE"), D("q2"), OP.add)
         else:
             for i in range(3):
                 cp(D("BASE", 20 * i, 20 * i + 20), d_(0, "BASE", 40 - 20 * i, 60 - 20 * i))
         ts(D("VV", 60, 80), D("BASE", 40, 60), sc(4), OP.add)
-        ts(D("E", 20, 40), ix(16, 36), 0.0, OP.mult, sc(3), OP.add)
-        ts(D("t1"), ix(16, 36), sc(0), OP.add)
-        ts(D("JS"), D("t1"), 4400, OP.add)
-        ts(D("t2"), D("t1"), sc(2), OP.subtract)
-        ts(D("t3"), D("t2"), 0.0, OP.is_lt, 3200, OP.mult)
-        ts(D("t4"), D("t2"), 800, OP.add)
-        tt(D("JR"), D("t3"), D("t4"), OP.add)
 
     def early(d):
         D = lambda n, a=0, b=None: d_(d, n, a, b)
         P = lambda r, k=1: d_(d, "P", 20 * r, 20 * r + 20 * k)
-        ops = [lambda r=r: ts(P(r), D("KO"), r, OP.logical_shift_right, 1, OP.bitwise_and) for r in range(6)]
+        ops = [lambda r=r: ts(P(r), D("KO"), r, OP.logical_shift_right, LW, OP.bitwise_and) for r in range(6)]
         return ops + [
-            lambda: ts(D("k7"), D("KO"), 7, OP.bitwise_and),
+            lambda: ts(D("k7"), D("KO"), 7 * LW, OP.bitwise_and),
             lambda: tt(D("s12"), P(1), P(2), OP.add),
-            lambda: ts(D("t5"), P(3, 3), 400, OP.mult),
-            lambda: ts(D("t2"), P(1), 2000, OP.mult),
-            lambda: ts(D("t3"), P(0), -800, OP.mult),
-            lambda: ts(D("n2"), P(5), sc(3), OP.is_equal),
-            lambda: cp(D("E", 0, 20), P(5)),
+            lambda: ts(D("t2"), P(1), -3, OP.mult),
+            lambda: ts(D("t3"), P(0), -2, OP.mult),
+            lambda: ts(D("n2"), P(5), sc(4), OP.is_equal),
             lambda: ts(D("fB", 0, 20), P(2), A("KC", 2, 3), OP.is_equal),
             lambda: tt(D("cnt"), D("s12"), P(0), OP.add),
-            lambda: tt(D("VV", 0, 60), D("t5"), D("BASE"), OP.add),
+            lambda: tt(D("VV", 0, 60), P(3, 3), D("BASE"), OP.add),
             lambda: ts(D("f0"), D("k7"), A("KC", 0, 1), OP.is_equal),
             lambda: ts(D("f1", 0, 20), D("s12"), A("KC", 1, 2), OP.is_equal),
-            lambda: ts(D("nb"), D("s12"), 1.0, OP.is_equal),
+            lambda: ts(D("nb"), D("s12"), LW, OP.is_equal),
             lambda: tt(D("t4"), D("t2"), D("t3"), OP.add),
-            lambda: ts(D("t1"), D("cnt"), -800, OP.mult),
-            lambda: ts(D("fB", 20, 40), D("n2"), -1.0, OP.mult, 1.0, OP.add),
+            lambda: ts(D("t1"), D("cnt"), -2, OP.mult),
+            lambda: ts(D("fB", 20, 40), P(5), sc(4), OP.not_equal),
             lambda: tt(D("f1", 20, 40), D("n2"), D("nb"), OP.mult),
-            lambda: tt(D("OR1", 20, 40), D("t4"), D("JR"), OP.add),
-            lambda: tt(D("OR0"), D("t1"), D("JS"), OP.add),
+            lambda: tt(D("OR1", 20, 40), D("t4"), sj(1), OP.add),
+            lambda: tt(D("OR0"), D("t1"), sj(0), OP.add),
             lambda: tt(D("t6"), D("VV", 0, 20), D("OR0"), OP.subtract),
             lambda: tt(D("t7"), D("t6"), D("f0"), OP.mult),
             lambda: tt(D("OR1", 0, 20), D("t7"), D("OR0"), OP.add),
@@ -431,25 +429,23 @@ def rank_program(g, core, T, topo):
         sh, an = OP.logical_shift_right, OP.bitwise_and
         spread(A("SCK", 0, 960), A("MK", 0, 960), 960)
         cp(D("KG"), A("SCK", 15, 960, 16))
-        ts(D("c0x"), x, 3, sh, 1, an)
-        ts(D("gb"), D("KG"), 1, an)
-        ts(D("yb1"), y, 1, sh, 1, an)
-        ts(D("c0y"), y, 3, sh, 1, an)
-        for h in (0, 20):
-            ts(D("c0z", h, h + 20), z, 3, sh, 1, an)
-            ts(D("c1y", h, h + 20), y, 4, sh, 1, an)
+        ts(D("c0x"), x, 3, sh, LW, an)
+        ts(D("gb"), D("KG"), LW, an)
+        ts(D("yb1"), y, 1, sh, LW, an)
+        ts(D("c0y"), y, 3, sh, LW, an)
+        ts(D("c0z"), z, 3, sh, LW, an)
+        ts(D("c1y"), y, 4, sh, LW, an)
         tt(D("m1"), D("c0x"), D("P", 80, 100), OP.is_equal)
-        ts(D("t8"), D("gb", 0, 40), 2800, OP.mult)
         tt(D("ne"), D("gb", 40, 60), D("yb1"), OP.not_equal)
-        ts(D("tb"), D("gb", 40, 60), 2000, OP.mult)
-        ts(D("tc"), D("c0y"), 400, OP.mult)
-        tt(D("mz"), D("c0z"), D("E"), OP.is_equal)
-        tt(D("my"), D("c1y"), D("E"), OP.is_equal)
-        tt(D("X"), D("t8", 0, 20), D("ST", 0, 20), OP.add)
+        ts(D("tb"), D("gb", 40, 60), -3, OP.mult)
+        for m, c in (("mz", "c0z"), ("my", "c1y")):
+            tt(D(m, 0, 20), D(c), D("P", 100, 120), OP.is_equal)
+            ts(D(m, 20, 40), D(c), sc(4), OP.is_equal)
+        tt(D("X"), D("ST", 0, 20), D("gb", 0, 20), OP.subtract)
         for h in (0, 20):
-            tt(D("ZZ", h, h + 20), D("t8", 20, 40), D("ST", 20, 40), OP.add)
+            tt(D("ZZ", h, h + 20), D("ST", 20, 40), D("gb", 20, 40), OP.subtract)
         tt(D("oe"), D("tb"), D("ST", 40, 60), OP.add)
-        tt(D("on"), D("tc"), D("ST", 60, 80), OP.add)
+        tt(D("on"), D("c0y"), D("ST", 60, 80), OP.add)
         tt(D("t9"), D("X"), V1, OP.subtract)
         tt(D("tf"), D("ZZ"), D("VV", 40, 80), OP.subtract)
         tt(D("td"), D("on"), D("oe"), OP.subtract)
@@ -470,24 +466,23 @@ def rank_program(g, core, T, topo):
         tt(D("u4"), D("v2"), D("OR1"), OP.subtract)
         tt(D("u5"), D("u4"), D("fB"), OP.mult)
         tt(D("RES"), D("u3"), D("u5"), OP.add)
-        ts(D("u6"), D("RES"), 3200, OP.is_ge, -3200, OP.mult)
-        tt(D("RS2"), D("RES"), D("u6"), OP.add)
-        cp(A("LU%d" % d, 0, 40), D("RS2"))
+        ts(D("RSM"), D("RES"), 8 * LW - 1, an)
+        cp(A("LU%d" % d, 0, 40), D("RSM"))
 
     def lookup(d, table, out, scalar_only=False):
-        a = (A(out, 0, 320), IND(A(table, 0, 8 * C), A("LU%d" % d, 0, 20)))
+        a = (A(out, 0, 320), IND(A(table, 0, 8 * LW), A("LU%d" % d, 0, 20)))
         if scalar_only:
             act(*a)
         else:
             cp(*a)
-        act(A(out, 320, 640), IND(A(table, 0, 8 * C), A("LU%d" % d, 20, 40)))
+        act(A(out, 320, 640), IND(A(table, 0, 8 * LW), A("LU%d" % d, 20, 40)))
 
     def offsets(out, d, flat, cm, cols):
         n = cols // 16
         tt(A("MG", 0, cols), IND(A(flat, 0, 640), A(cm, 0, n)), A("MASK", 0, cols), OP.mult)
         spread(A("SN", 0, cols), A("MG", 0, cols), cols)
         ts(d_(d, "u1", 0, n), A("SN", 15, cols, 16), sc(2), OP.subtract)
-        ts(d_(d, "u2", 0, n), d_(d, "u1", 0, n), 0.0, OP.is_lt, 3200, OP.mult)
+        ts(d_(d, "u2", 0, n), d_(d, "u1", 0, n), 0.0, OP.is_lt, 8 * C, OP.mult)
         tt(d_(d, "u3", 0, n), d_(d, "u1", 0, n), d_(d, "u2", 0, n), OP.add)
         for t in (2, 3, 0, 1):
             ts(A(out, 26 * t, 26 * t + n), d_(d, "u3", 0, n), 4, OP.mult, t, OP.add)
@@ -500,39 +495,51 @@ def rank_program(g, core, T, topo):
             else:
                 cp(*a)
 
-    def scores(src):
+    def scores(src, first=None, second=None):
         quant("QX", 0, ST, A(src, 0, 4 * ST))
         for n, c0 in enumerate((0, 128, 192)):
             mm(A("PS", 512 * n, 512 * n + 128), A("QX", c0, c0 + 128), A("SX", c0, c0 + 128), A("QUP", 0, 128), A("SUP", 0, 128))
+        if first:
+            first()
         for n in range(3):
             h = 16 if n == 2 else 0
             for s in (0, 32):
                 o = 8 * s + 32 * n
                 tt(A("BT", o, o + 32 - h), A("PS", 512 * n + s + h, 512 * n + s + 32), A("THR", s + h, s + 32), OP.is_gt)
         quant("QB", 0, 192, A("BT", 0, 768))
+        if second:
+            second()
         for d in range(2):
             for i in range(2):
                 k = 256 * d + 128 * i
-                mm(A("PS", 1536 + 512 * d, 1664 + 512 * d), A("QK", k, k + 128), A("SK", k, k + 128), A("QB", 64 * i, 64 * i + 128), A("SB", 64 * i, 64 * i + 128), i == 0, i == 1)
+                mm(A("PS", 1536 + 2048 * d, 1664 + 2048 * d), A("QK", k, k + 128), A("SK", k, k + 128), A("QB", 64 * i, 64 * i + 128), A("SB", 64 * i, 64 * i + 128), i == 0, i == 1)
         cp(A("KU0", 0, 20), A("PS", 1536, 1556))
-        cp(d_(0, "KO"), A("PS", 1536, 1556))
-        act(A("KF0", 0, 320), IND(A("IDT", 0, 512), A("KU0", 0, 20)))
-        ts(A("KU1", 0, 20), A("PS", 2048, 2068), 7.0, OP.add)
-        ts(d_(1, "KO"), A("PS", 2048, 2068), 7.0, OP.add)
+        ts(d_(0, "KO"), A("PS", 1536, 1556), LW, OP.mult)
+        act(A("KF0", 0, 320), IND(A("IDT", 0, 512), A("KU0", 0, 20)), scale=512.0)
 
+    def back_signs():
+        ts(A("KU1", 0, 20), A("PS", 3584, 3604), 7.0, OP.add)
+        ts(d_(1, "KO"), A("PS", 3584, 3604), 7, OP.add, LW, OP.mult)
+        act(A("KF1", 0, 320), IND(A("IDT", 0, 512), A("KU1", 0, 20)), scale=512.0)
+
+    statics(0)
     quant("QU", 0, 128, A("UT", 0, 512))
     emit("v", V.tensor_copy, 1, CW("QUP", 0, 128), IND(CW("QU", 0, 128), A("UL", 0, 8)))
     act(A("SUP", 0, 128), IND(A("SU", 0, 128), A("UL", 0, 8)))
     quant("QK", 0, 512, A("KWT", 0, 2048))
-    statics(0)
-    emit("v", V.tensor_copy, 1, IND(A("QQ", 640, 960), A("LNU", 40, 60)), A("IDT", 0, 320))
-    scores("R")
     act(A("MF", 0, 320), A("IDT", 0, 320), scale=1025.0)
-    ts(A("ML", 0, 80), IND(A("QQ", 640, 960), A("CLU", 0, 5)), 320.0, OP.add)
-    ts(A("ML", 80, 160), IND(A("QQ", 0, 320), A("CLU", 0, 5)), 320.0, OP.add)
-    ts(A("ML", 160, 240), A("ML", 80, 160), 1024.0, OP.mult)
-    tt(A("MF", 320, 400), A("ML", 160, 240), A("ML", 0, 80), OP.add)
-    emit("v", V.tensor_copy, 1, IND(A("CF", 0, 400), A("PU", 0, 25)), A("MF", 0, 400))
+
+    def inverse2():
+        emit("v", V.tensor_copy, 1, IND(A("QQ", 640, 960), A("LNU", 40, 60)), A("IDT", 0, 320))
+
+    def columns():
+        ts(A("ML", 0, 80), IND(A("QQ", 640, 960), A("CLU", 0, 5)), 320.0, OP.add)
+        ts(A("ML", 80, 160), IND(A("QQ", 0, 320), A("CLU", 0, 5)), 320.0, OP.add)
+        ts(A("ML", 160, 240), A("ML", 80, 160), 1024.0, OP.mult)
+        tt(A("MF", 320, 400), A("ML", 160, 240), A("ML", 0, 80), OP.add)
+        emit("v", V.tensor_copy, 1, IND(A("CF", 0, 400), A("PU", 0, 25)), A("MF", 0, 400))
+
+    scores("R", inverse2, columns)
     tt(A("MG", 0, 400), A("CF", 0, 400), A("MASK", 0, 400), OP.mult)
     spread(A("SN", 0, 400), A("MG", 0, 400), 400)
     cp(ix(64, 89), A("SN", 15, 400, 16))
@@ -601,7 +608,7 @@ def rank_program(g, core, T, topo):
             for f in meanwhile:
                 f()
 
-        act(A("KF1", 0, 320), IND(A("IDT", 0, 512), A("KU1", 0, 20)))
+        back_signs()
         layer(KX, C, C - KX, "RL", 304, early(1) if r else [])
         shifted("d_ye%d" % r, "y", "R", 4 * C, T.R, 4 * KX, 4 * C, [A("R", 4 * KX, 4 * C)])
         if r == 0:
@@ -618,7 +625,7 @@ def rank_program(g, core, T, topo):
         if r < STEPS - 1:
             act(A("TN", 0, ST), A("FL1", 0, ST))
             act(A("TN", ST, C), IND(A("FL1", 0, 640), A("LTL", 0, 5)))
-            shifted("d_tn%d" % r, "y", "TN", C, T.TN, 0, C, [A("TN", 0, C)])
+            shifted("d_tn%d" % r, "y", "TN", LW, T.TN, 0, C, [A("TN", 0, C)])
         else:
             lookup(0, "T0", "FLO", True)
             act(A("OPF", 0, C), IND(A("FLO", 0, 640), A("CM0", 0, 25)))

from concourse.mybir import dt, AluOpType, ActivationFunctionType

C, ST, KX, STEPS, N = 400, 320, 96, 3, 8
MATES = [1, 2, 4]
W8 = 8 * 4 * C
LW = 512
OP = AluOpType
COPY, RELU = ActivationFunctionType.Copy, ActivationFunctionType.Relu
CODES = "float8_e4m3fn_x4"

SCRATCH = {
    "R": ("sbuf", [128, W8], "bfloat16"), "XT": ("sbuf", [128, 4 * C], "bfloat16"), "ZT": ("sbuf", [128, 4 * C], "bfloat16"),
    "UT": ("sbuf", [128, 512], "bfloat16"), "VT": ("sbuf", [128, 512], "bfloat16"),
    "ET": ("sbuf", [128, 2048], "bfloat16"), "ONE": ("sbuf", [128, 512], "bfloat16"),
    "KWT": ("sbuf", [128, 2048], "bfloat16"), "BT": ("sbuf", [128, 768], "bfloat16"),
    "LP": ("sbuf", [128, 25], "int32"), "LN": ("sbuf", [128, 60], "int32"),
    "PU": ("sbuf", [128, 26], "uint16"), "LNU": ("sbuf", [128, 60], "uint16"),
    "LOF0": ("sbuf", [128, 60], "uint16"), "LOF1": ("sbuf", [128, 60], "uint16"),
    "LX0": ("sbuf", [128, 60], "uint16"), "LX1": ("sbuf", [128, 60], "uint16"),
    "CM0": ("sbuf", [128, 26], "uint16"), "CM1": ("sbuf", [128, 26], "uint16"), "LTL": ("sbuf", [128, 6], "uint16"),
    "UL": ("sbuf", [128, 8], "uint16"), "CLU": ("sbuf", [128, 6], "uint16"),
    "KU0": ("sbuf", [128, 20], "uint16"), "KU1": ("sbuf", [128, 20], "uint16"),
    "LU0": ("sbuf", [128, 40], "uint16"), "LU1": ("sbuf", [128, 40], "uint16"),
    "OFZ": ("sbuf", [128, 104], "uint16"), "OFX": ("sbuf", [128, 104], "uint16"),
    "IQ": ("sbuf", [128, 960], "bfloat16"), "MASK": ("sbuf", [128, 960], "bfloat16"), "SEG": ("sbuf", [128, 960], "bfloat16"),
    "IDT": ("sbuf", [128, 512], "float32"), "ID5": ("sbuf", [128, 320], "float32"), "GI": ("sbuf", [128, 64], "bfloat16"),
    "THR": ("sbuf", [128, 64], "float32"), "IDX": ("sbuf", [128, 128], "int32"), "SC": ("sbuf", [128, 24], "float32"),
    "SJ": ("sbuf", [128, 60], "float32"), "KC": ("sbuf", [128, 3], "float32"),
    "QQ": ("sbuf", [128, 1280], "float32"), "VA": ("sbuf", [128, 640], "float32"), "MF": ("sbuf", [128, 400], "float32"), "ML": ("sbuf", [128, 240], "float32"),
    "CF": ("sbuf", [128, 400], "float32"), "MG": ("sbuf", [128, 960], "float32"), "SN": ("sbuf", [128, 960], "float32"),
    "KF0": ("sbuf", [128, 320], "bfloat16"), "KF1": ("sbuf", [128, 320], "bfloat16"),
    "MK": ("sbuf", [128, 960], "bfloat16"), "SCK": ("sbuf", [128, 960], "bfloat16"),
    "DF0": ("sbuf", [128, 2048], "float32"), "DF1": ("sbuf", [128, 2048], "float32"),
    "DI0": ("sbuf", [128, 704], "int32"), "DI1": ("sbuf", [128, 704], "int32"),
    "T0": ("sbuf", [128, 8 * LW], "float32"), "TN": ("sbuf", [128, 8 * LW], "float32"),
    "FL0": ("sbuf", [128, 640], "float32"), "FL1": ("sbuf", [128, 640], "float32"), "FLO": ("sbuf", [128, 640], "float32"),
    "OPF": ("sbuf", [128, 400], "float32"), "RL": ("sbuf", [128, 1216], "float32"), "RL2": ("sbuf", [128, 512], "float32"), "YO": ("sbuf", [128, 400], "float32"),
    "PS": ("psum", [128, 4096], "float32"),
}
for _n, _w in (("U", 128), ("UP", 128), ("V", 128), ("W", 512), ("E", 512), ("K", 512), ("B", 192), ("X", C), ("S", 128), ("R", KX)):
    SCRATCH["Q" + _n] = ("sbuf", [128, _w], CODES)
    SCRATCH["S" + _n] = ("sbuf", [128, _w], "uint8")
for _r in range(STEPS):
    SCRATCH["HQ%d" % _r] = ("sbuf", [128, C], CODES)
    SCRATCH["HS%d" % _r] = ("sbuf", [128, C], "uint8")
DMAS = ["d_ln", "d_p", "d_u", "d_x", "d_xs", "d_v", "d_w", "d_t0", "d_tn0", "d_tn1", "d_out", "d_op"]
DMAS += ["d_%s%d" % (k, r) for k in ("ye", "yl") for r in range(STEPS)]
SEMAPHORES = ["ev", "es", "et", "eg", "rarr", "rsent"] + DMAS + ["arr%d" % r for r in range(STEPS)] + ["snt%d" % r for r in range(STEPS)]


def hops(T, topo, i, r):
    src, dst = T.cores[i], T.cores[i ^ MATES[r]]
    if topo.may_write(src, dst):
        return None, None
    c = [k for k in topo.cores_of(src) if k not in T.cores and topo.die(k) == topo.die(src) and topo.may_write(k, dst)]
    return c[0], c[-1]


def mask_of(topo, src, dst):
    e = topo.engines(src, dst)[:8]
    return sum(1 << k for k in e), len(e)


def relay(g, core, T, topo):
    for i in range(N):
        for r in range(STEPS):
            pair = hops(T, topo, i, r)
            if core not in pair:
                continue
            src, dst = T.cores[i], T.cores[i ^ MATES[r]]
            jobs = [k for k in range(2) if pair[k] == core]
            n_in = mask_of(topo, src, core)[1]
            m, n = mask_of(topo, core, dst)
            rid, pid = topo.addr(dst, core)
            g.wait_ge(T.sem.rarr, n_in * len(jobs))
            for k in jobs:
                if k == 0:
                    o, s = T["HQ%d" % r][:, 0:KX].bitcast(dt.uint8), T.QR[:, 0:KX].bitcast(dt.uint8)
                else:
                    o, s = T["HS%d" % r][:, 0:KX], T.SR[:, 0:KX]
                g.remote_dma(out_ap=o, in_ap=s, remote_sem=T.sem["arr%d" % r], local_sem=T.sem.rsent, pid=pid, routing_id=rid, dma_engine_mask=m)
            g.wait_ge(T.sem.rsent, n * len(jobs))


def A(name, a, b, s=1):
    return ("A", name, a, b, s)


def IND(win, off):
    return ("I", win, off)


def CW(name, a, b):
    return ("C", name, a, b, 1)


def is_ap(x):
    return isinstance(x, tuple) and len(x) > 0 and x[0] in ("A", "I", "C")


def builder(g, T):
    Q = {"v": g.vector, "s": g.scalar, "t": g.tensor, "g": g, "y": g.sync}
    known = {q: {} for q in Q}
    total, clock, hist, waited, pending = {}, {}, {}, {}, {}

    def ap(x):
        if x[0] == "A":
            _, n, a, b, s = x
            return T[n][:, a:b] if s == 1 else T[n][:, a:b:s]
        if x[0] == "C":
            return T[x[1]][:, x[2]:x[3]].bitcast(dt.uint32)
        return ap(x[1]).indirect(ap(x[2]))

    def region(x):
        _, n, a, b, s = x
        if n == "PS":
            return n, (a // 512 * 512, (b + 511) // 512 * 512, 1)
        return n, (a, b, s)

    def meet(p, q):
        if p[1] <= q[0] or q[1] <= p[0]:
            return False
        return not (p[2] == q[2] > 1 and (p[0] - q[0]) % p[2])

    def wait(q, evs):
        best = {}
        for s, v in set(evs):
            if known[q].get(s, 0) < v:
                best[s] = max(v, best.get(s, 0))
        evs = [e for e in best.items() if not any(o != e[0] and clock[(o, w)].get(e[0], 0) >= e[1] for o, w in best.items())]
        for s, v in sorted(evs):
            Q[q].wait_ge(T.sem[s], v)
            waited[s] = max(v, waited.get(s, 0))
            for k, w in clock[(s, v)].items():
                known[q][k] = max(w, known[q].get(k, 0))

    def hazards(q, reads, writes, acc=False):
        evs = []
        for x, w in [(r, False) for r in reads] + [(r, True) for r in writes]:
            n, reg = region(x)
            for reg2, w2, ev, q2 in hist.get(n, []):
                if meet(reg, reg2) and (w or w2 or (n == "PS" and q2 != q)) and not (acc and q2 == q):
                    evs.append(ev)
        wait(q, evs)

    def note(q, reads, writes, ev):
        for x, w in [(r, False) for r in reads] + [(r, True) for r in writes]:
            n, reg = region(x)
            h = hist.setdefault(n, [])
            if w and reg[2] == 1:
                h[:] = [e for e in h if not (reg[0] <= e[0][0] and e[0][1] <= reg[1])]
            h[:] = [e for e in h if not (e[0] == reg and e[1] == w and e[3] == q and e[2][0] == ev[0])]
            h.append((reg, w, ev, q))

    def parts(xs):
        out = []
        for x in xs:
            if is_ap(x):
                out += [("A",) + x[1][1:], x[2]] if x[0] == "I" else [("A",) + x[1:]]
        return out

    def emit(q, fn, nout, *args, acc=False, **kw):
        writes, reads = [], parts(args[nout:]) + parts(kw.values())
        for x in args[:nout]:
            if x[0] == "I":
                writes.append(("A",) + x[1][1:])
                reads.append(x[2])
            else:
                writes.append(("A",) + x[1:])
        hazards(q, reads, writes, acc)
        s = "e" + q
        i = fn(*[ap(x) if is_ap(x) else x for x in args], **{k: ap(x) if is_ap(x) else x for k, x in kw.items()})
        i.then_inc(T.sem[s], 1)
        total[s] = total.get(s, 0) + 1
        c = dict(known[q])
        c[s] = total[s]
        clock[(s, total[s])] = c
        note(q, reads, writes, (s, total[s]))

    def batch(sem, q, reads, writes):
        o = pending.setdefault(sem, [[], [], {}])
        o[0] += list(reads)
        o[1] += list(writes)
        for k, v in known[q].items():
            o[2][k] = max(v, o[2].get(k, 0))

    def dma(q, sem, out, in_, reads=(), writes=()):
        hazards(q, reads, writes)
        Q[q].dma_start(out, in_).then_inc(T.sem[sem], 16)
        total[sem] = total.get(sem, 0) + 16
        batch(sem, q, reads, writes)

    def close(sem):
        reads, writes, c = pending.pop(sem)
        c[sem] = total[sem]
        clock[(sem, total[sem])] = c
        note("dma", reads, writes, (sem, total[sem]))

    def remote(out, in_, reads, rsem, lsem, addr, m, n):
        hazards("g", reads, [])
        g.remote_dma(out_ap=out, in_ap=in_, remote_sem=T.sem[rsem], local_sem=T.sem[lsem], pid=addr[1], routing_id=addr[0], dma_engine_mask=m)
        total[lsem] = total.get(lsem, 0) + n
        batch(lsem, "g", reads, [])

    def arrives(writes, sem, n):
        total[sem] = n
        clock[(sem, n)] = {sem: n}
        note("remote", [], writes, (sem, n))

    def finish():
        for s in sorted(total):
            if waited.get(s, 0) < total[s]:
                g.wait_ge(T.sem[s], total[s])

    return emit, dma, close, remote, arrives, finish


def rank_program(g, core, T, topo):
    rank = T.rank_of(core)
    if rank is None:
        relay(g, core, T, topo)
        return
    emit, dma, close, remote, arrives, finish = builder(g, T)
    V, S = g.vector, g.scalar

    def ts(out, x, s1, op0, s2=None, op1=None):
        if op1 is None:
            emit("v", V.tensor_scalar, 1, out, x, s1, None, op0)
        else:
            emit("v", V.tensor_scalar, 1, out, x, s1, s2, op0, op1)

    def tt(out, x, y, op):
        emit("v", V.tensor_tensor, 1, out, x, y, op)

    def cp(out, x):
        emit("v", V.tensor_copy, 1, out, x)

    def act(out, x, func=COPY, **kw):
        emit("s", S.activation, 1, out, x, func, **kw)

    def quant(n, a, b, x, sn=None):
        emit("v", V.quantize_mx, 2, A(n, a, b), A(sn or "S" + n[1:], a, b), x)

    def mm(out, l, ls, r, rs, start=True, stop=True):
        emit("t", g.tensor.matmul_mx, 1, out, l, ls, r, rs, start, stop, acc=not start)

    def iota(out, pattern, base, cm, whole=False):
        if whole:
            emit("g", g.iota, 1, out, pattern, base, cm)
        else:
            emit("g", g.iota, 1, out, pattern, base, cm, allow_small_or_imprecise_dtypes=True)

    def sc(i):
        return A("SC", i, i + 1)

    def ix(a, b):
        return A("IDX", a, b)

    def sj(i):
        return A("SJ", 20 * i, 20 * i + 20)

    def shifted(sem, queues, name, width, src, a, b, reads):
        n = 0
        for k in range(1, 8):
            for d0, s0, rows in ((0, 16 * k, 128 - 16 * k), (128 - 16 * k, 0, 16 * k)):
                dma(queues[n % len(queues)], sem, T[name][d0:d0 + rows, width * k + a:width * k + b], src[s0:s0 + rows, a:b],
                    reads=reads, writes=[A(name, width * k + a, width * k + b)])
                n += 1
        close(sem)

    for k in range(8):
        dma("sy"[k % 2], "d_ln", T.LN[16 * k:16 * k + 16, :], T.ln[:, :], writes=[A("LN", 0, 60)])
    close("d_ln")
    dma("s", "d_p", T.LP[:, :], T.p[:, :], writes=[A("LP", 0, 25)])
    close("d_p")
    dma("y", "d_u", T.UT[:, :], T.u[:, :], writes=[A("UT", 0, 512)])
    close("d_u")
    dma("y", "d_x", T.R[:, 0:4 * C], T.x[:, :], writes=[A("R", 0, 4 * C)])
    close("d_x")

    iota(ix(0, 1), [[0, 1]], 0, 1, True)
    iota(A("GI", 0, 64), [[0, 2], [1, 8], [0, 4]], 0, 0)
    iota(ix(16, 36), [[16, 20]], 0, 0, True)
    iota(ix(36, 41), [[64, 5]], 0, 0, True)
    iota(ix(48, 56), [[0, 8]], 0, 0, True)
    iota(A("IDT", 0, 512), [[1, 512]], 0, 0)
    iota(A("ID5", 0, 320), [[512, 320]], 0, 0)
    iota(A("IQ", 0, 960), [[0, 60], [1, 16]], 0, 0)
    for i, k in enumerate((1536.0, -512.0, 512.0)):
        emit("v", V.memset, 1, A("KC", i, i + 1), k)
    iota(A("ONE", 0, 512), [[0, 512]], 1, 0)
    iota(A("BT", 0, 768), [[0, 768]], 0, 0)
    for i, seq in enumerate((((16, -1), (32, 7), (48, -1), (80, 0), (96, -1), (112, 4)), ((16, 2), (32, -1), (96, 0), (112, -1)), ((16, -1), (112, 0)))):
        for p0, k in seq:
            emit("g", g.affine_select, 1, A("KC", i, i + 1), A("KC", i, i + 1), [[0, 1]], OP.is_gt, 512.0 * k, p0, -1)
    for b in range(4):
        emit("g", g.affine_select, 1, A("ET", 512 * b, 512 * b + 512), A("ONE", 0, 512), [[-1, 512]], OP.is_equal, 0.0, b, 4)
    for n in ("T0", "TN"):
        for k in range(8):
            iota(A(n, LW * k + C, LW * k + LW), [[0, LW - C]], 0, 0)

    ts(ix(1, 2), ix(0, 1), 15, OP.bitwise_and)
    ts(ix(2, 3), ix(0, 1), 4, OP.logical_shift_right)
    ts(ix(3, 4), ix(0, 1), 5, OP.logical_shift_right)
    ts(ix(4, 5), ix(0, 1), 3, OP.bitwise_and)
    ts(ix(5, 6), ix(0, 1), 4, OP.logical_shift_right, 1, OP.bitwise_and)
    cp(sc(0), ix(1, 2))
    cp(sc(1), ix(2, 3))
    ts(sc(2), ix(2, 3), 400, OP.mult)
    ts(sc(4), ix(5, 6), LW, OP.mult)
    ts(sc(12), ix(2, 3), LW, OP.mult, -8192, OP.add)
    cp(sc(9), ix(3, 4))
    ts(sc(5), ix(4, 5), 3, OP.is_equal, -47, OP.mult)
    ts(sc(6), ix(4, 5), 16, OP.mult)
    tt(sc(7), sc(6), sc(5), OP.add)
    ts(sc(8), sc(6), 17, OP.add)
    ts(sc(10), sc(0), 4, OP.mult)
    tt(sc(11), sc(10), sc(9), OP.add)
    ts(sj(2), ix(16, 36), sc(0), OP.add)
    ts(sj(0), sj(2), 9728, OP.add)
    ts(sj(1), sj(2), sc(12), OP.subtract, 1024, OP.add)

    cp(A("PU", 0, 25), A("LP", 0, 25))
    act(A("T0", 0, C), IND(A("IDT", 0, 512), A("PU", 0, 25)), ActivationFunctionType.Identity, bias=sc(2))
    shifted("d_t0", "y", "T0", LW, T.T0, 0, C, [A("T0", 0, C)])
    shifted("d_xs", "y", "R", 4 * C, T.x, 0, 4 * C, [])
    dma("y", "d_w", T.QW[:, :].bitcast(dt.uint8), T.wc[:, :], writes=[A("QW", 0, 512)])
    dma("y", "d_w", T.SW[:, :], T.ws[:, :], writes=[A("SW", 0, 512)])
    close("d_w")
    dma("y", "d_v", T.VT[:, :], T.v[:, :], writes=[A("VT", 0, 512)])
    close("d_v")

    cp(A("LNU", 0, 60), A("LN", 0, 60))
    emit("v", V.tensor_copy, 1, IND(A("QQ", 0, 320), A("LNU", 0, 20)), A("IDT", 0, 320))
    tt(A("VA", 0, 320), IND(A("ID5", 0, 320), A("LNU", 0, 20)), A("IDT", 0, 320), OP.add)
    cp(A("LOF0", 0, 40), A("LN", 20, 60))
    ts(A("LOF0", 40, 60), A("LN", 40, 60), 320, OP.add)
    emit("v", V.tensor_copy, 1, IND(A("QQ", 320, 640), A("LNU", 20, 40)), A("VA", 0, 320))
    ts(A("MASK", 0, 960), A("IQ", 0, 960), sc(0), OP.is_equal)
    act(A("SEG", 0, 960), A("IQ", 0, 960), ActivationFunctionType.Sign)
    ts(A("THR", 0, 64), A("GI", 0, 64), sc(1), OP.not_equal, 1.0e29, OP.mult)
    ts(A("UL", 0, 8), ix(48, 56), sc(7), OP.add)
    ts(A("UL", 2, 4), ix(48, 50), sc(8), OP.add)
    ts(A("CLU", 0, 5), ix(36, 41), sc(11), OP.add)
    for i, ws in enumerate(((1, 2, 4, 8), (16, 32, 0, 0), (-4, -2, -1, 32), (16, 8, 0, 0))):
        for t in range(4):
            act(A("KWT", 512 * i + t, 512 * i + 512, 4), A("MASK", 0, 128), scale=float(ws[t]))

    def spread(out, in_, n):
        emit("v", V.tensor_tensor_scan, 1, out, A("SEG", 0, n), in_, 0.0, OP.mult, OP.add)

    off = {}
    for buf, pairs in (
        ("DF", [("ST", 80), ("BASE", 60), ("VV", 80), ("OR0", 20), ("OR1", 40), ("f0", 20), ("f1", 40), ("fB", 40), ("s12", 20), ("cnt", 20),
                ("t1", 20), ("t2", 20), ("t3", 20), ("t4", 20), ("n2", 20), ("nb", 20), ("t6", 20), ("t7", 20),
                ("X", 20), ("ZZ", 40), ("m1", 20), ("t9", 20), ("ta", 20), ("v1", 40), ("ne", 20), ("tb", 20), ("oe", 20), ("on", 20),
                ("td", 20), ("te", 20), ("o1", 40), ("mz", 40), ("tf", 40), ("tg", 40), ("w", 40), ("my", 40), ("th", 40), ("ti", 40), ("v2", 40),
                ("u1", 40), ("u2", 40), ("u3", 40), ("u4", 40), ("u5", 40), ("q3", 60), ("q4", 60)]),
        ("DI", [("P", 120), ("k7", 20), ("KG", 60), ("gb", 60), ("c0x", 20), ("c0y", 20), ("c0z", 20), ("c1y", 20), ("yb1", 20), ("KO", 20),
                ("a1", 60), ("a2", 60), ("pk", 20), ("pa", 20), ("pr", 20), ("pb", 20), ("RES", 40), ("RSM", 40)])):
        at = 0
        for n, w in pairs:
            off[n] = (buf, at, w)
            at += w

    def d_(d, n, a=0, b=None):
        buf, at, w = off[n]
        return A("%s%d" % (buf, d), at + a, at + (w if b is None else b))

    def statics(d):
        D = lambda n, a=0, b=None: d_(d, n, a, b)
        tt(A("MG", 0, 960), IND(A("QQ", 0, 640 if d == 0 else 1280), A("LOF%d" % d, 0, 60)), A("MASK", 0, 960), OP.mult)
        spread(A("SN", 0, 960), A("MG", 0, 960), 960)
        cp(D("pk"), A("SN", 655, 960, 16))
        cp(A("LX%d" % d, 0, 40), A("SN", 15, 640, 16))
        ts(D("ST", 0, 40), A("SN", 15, 640, 16), sc(12), OP.subtract)
        ts(D("pa"), D("pk"), 511, OP.bitwise_and)
        ts(D("pr"), D("pk"), 9, OP.logical_shift_right, 3, OP.bitwise_and)
        ts(D("pb"), D("pk"), 11, OP.logical_shift_right)
        cp(A("LX%d" % d, 40, 60), D("pa"))
        ts(D("ST", 40, 60), D("pa"), sc(12), OP.subtract, LW, OP.add)
        ts(D("q3", 0, 20), D("pr"), 1024, OP.mult, 320, OP.add)
        ts(D("q4", 0, 20), D("pb"), sc(12), OP.subtract)
        tt(D("ST", 60, 80), D("q3", 0, 20), D("q4", 0, 20), OP.add)
        if d == 0:
            ts(D("a1"), A("LN", 0, 60), 3, OP.bitwise_and)
            ts(D("a2"), A("LN", 0, 60), 2, OP.logical_shift_right)
            ts(D("q3"), D("a1"), 1024, OP.mult, 320, OP.add)
            ts(D("q4"), D("a2"), sc(12), OP.subtract)
            tt(D("BASE"), D("q3"), D("q4"), OP.add)
        else:
            for i in range(3):
                cp(D("BASE", 20 * i, 20 * i + 20), d_(0, "BASE", 40 - 20 * i, 60 - 20 * i))
        ts(D("VV", 60, 80), D("BASE", 40, 60), sc(4), OP.add)

    def early(d):
        D = lambda n, a=0, b=None: d_(d, n, a, b)
        P = lambda r, k=1: d_(d, "P", 20 * r, 20 * r + 20 * k)
        ops = [lambda r=r: ts(P(r), D("KO"), r, OP.logical_shift_right, LW, OP.bitwise_and) for r in range(6)]
        return ops + [
            lambda: ts(D("k7"), D("KO"), 7 * LW, OP.bitwise_and),
            lambda: tt(D("s12"), P(1), P(2), OP.add),
            lambda: ts(D("t2"), P(1), -3, OP.mult),
            lambda: ts(D("t3"), P(0), -2, OP.mult),
            lambda: ts(D("n2"), P(5), sc(4), OP.is_equal),
            lambda: ts(D("fB", 0, 20), P(2), A("KC", 2, 3), OP.is_equal),
            lambda: tt(D("cnt"), D("s12"), P(0), OP.add),
            lambda: tt(D("VV", 0, 60), P(3, 3), D("BASE"), OP.add),
            lambda: ts(D("f0"), D("k7"), A("KC", 0, 1), OP.is_equal),
            lambda: ts(D("f1", 0, 20), D("s12"), A("KC", 1, 2), OP.is_equal),
            lambda: ts(D("nb"), D("s12"), LW, OP.is_equal),
            lambda: tt(D("t4"), D("t2"), D("t3"), OP.add),
            lambda: ts(D("t1"), D("cnt"), -2, OP.mult),
            lambda: ts(D("fB", 20, 40), P(5), sc(4), OP.not_equal),
            lambda: tt(D("f1", 20, 40), D("n2"), D("nb"), OP.mult),
            lambda: tt(D("OR1", 20, 40), D("t4"), sj(1), OP.add),
            lambda: tt(D("OR0"), D("t1"), sj(0), OP.add),
            lambda: tt(D("t6"), D("VV", 0, 20), D("OR0"), OP.subtract),
            lambda: tt(D("t7"), D("t6"), D("f0"), OP.mult),
            lambda: tt(D("OR1", 0, 20), D("t7"), D("OR0"), OP.add),
        ]

    def gather_k(d):
        tt(A("MK", 0, 960), IND(A("KF%d" % d, 0, 320), A("LX%d" % d, 0, 60)), A("MASK", 0, 960), OP.mult)

    def late(d):
        D = lambda n, a=0, b=None: d_(d, n, a, b)
        V1, x, z, y = D("VV", 20, 40), D("KG", 0, 20), D("KG", 20, 40), D("KG", 40, 60)
        sh, an = OP.logical_shift_right, OP.bitwise_and
        spread(A("SCK", 0, 960), A("MK", 0, 960), 960)
        cp(D("KG"), A("SCK", 15, 960, 16))
        ts(D("c0x"), x, 3, sh, LW, an)
        ts(D("gb"), D("KG"), LW, an)
        ts(D("yb1"), y, 1, sh, LW, an)
        ts(D("c0y"), y, 3, sh, LW, an)
        ts(D("c0z"), z, 3, sh, LW, an)
        ts(D("c1y"), y, 4, sh, LW, an)
        tt(D("m1"), D("c0x"), D("P", 80, 100), OP.is_equal)
        tt(D("ne"), D("gb", 40, 60), D("yb1"), OP.not_equal)
        ts(D("tb"), D("gb", 40, 60), -3, OP.mult)
        for m, c in (("mz", "c0z"), ("my", "c1y")):
            tt(D(m, 0, 20), D(c), D("P", 100, 120), OP.is_equal)
            ts(D(m, 20, 40), D(c), sc(4), OP.is_equal)
        tt(D("X"), D("ST", 0, 20), D("gb", 0, 20), OP.subtract)
        for h in (0, 20):
            tt(D("ZZ", h, h + 20), D("ST", 20, 40), D("gb", 20, 40), OP.subtract)
        tt(D("oe"), D("tb"), D("ST", 40, 60), OP.add)
        tt(D("on"), D("c0y"), D("ST", 60, 80), OP.add)
        tt(D("t9"), D("X"), V1, OP.subtract)
        tt(D("tf"), D("ZZ"), D("VV", 40, 80), OP.subtract)
        tt(D("td"), D("on"), D("oe"), OP.subtract)
        tt(D("ta"), D("t9"), D("m1"), OP.mult)
        tt(D("tg"), D("tf"), D("mz"), OP.mult)
        tt(D("te"), D("td"), D("ne"), OP.mult)
        for h in (0, 20):
            tt(D("v1", h, h + 20), D("ta"), V1, OP.add)
        tt(D("w"), D("tg"), D("VV", 40, 80), OP.add)
        for h in (0, 20):
            tt(D("o1", h, h + 20), D("te"), D("oe"), OP.add)
        tt(D("u1"), D("v1"), D("OR1"), OP.subtract)
        tt(D("th"), D("o1"), D("w"), OP.subtract)
        tt(D("u2"), D("u1"), D("f1"), OP.mult)
        tt(D("ti"), D("th"), D("my"), OP.mult)
        tt(D("u3"), D("u2"), D("OR1"), OP.add)
        tt(D("v2"), D("ti"), D("w"), OP.add)
        tt(D("u4"), D("v2"), D("OR1"), OP.subtract)
        tt(D("u5"), D("u4"), D("fB"), OP.mult)
        tt(D("RES"), D("u3"), D("u5"), OP.add)
        ts(D("RSM"), D("RES"), 8 * LW - 1, an)
        cp(A("LU%d" % d, 0, 40), D("RSM"))

    def lookup(d, table, out, scalar_only=False):
        a = (A(out, 0, 320), IND(A(table, 0, 8 * LW), A("LU%d" % d, 0, 20)))
        if scalar_only:
            act(*a)
        else:
            cp(*a)
        act(A(out, 320, 640), IND(A(table, 0, 8 * LW), A("LU%d" % d, 20, 40)))

    def offsets(out, d, flat, cm, cols):
        n = cols // 16
        tt(A("MG", 0, cols), IND(A(flat, 0, 640), A(cm, 0, n)), A("MASK", 0, cols), OP.mult)
        spread(A("SN", 0, cols), A("MG", 0, cols), cols)
        ts(d_(d, "u1", 0, n), A("SN", 15, cols, 16), sc(2), OP.subtract)
        ts(d_(d, "u2", 0, n), d_(d, "u1", 0, n), 0.0, OP.is_lt, 8 * C, OP.mult)
        tt(d_(d, "u3", 0, n), d_(d, "u1", 0, n), d_(d, "u2", 0, n), OP.add)
        for t in (2, 3, 0, 1):
            ts(A(out, 26 * t, 26 * t + n), d_(d, "u3", 0, n), 4, OP.mult, t, OP.add)

    def pull(dst, offs, c0, c1):
        for t in (2, 0, 3, 1):
            a = (A(dst, 4 * c0 + t, 4 * c1, 4), IND(A("R", 0, W8), A(offs, 26 * t + c0 // 16, 26 * t + c1 // 16)))
            if t >= 2:
                act(*a)
            else:
                cp(*a)

    def scores(src, first=None, second=None):
        quant("QX", 0, ST, A(src, 0, 4 * ST))
        for n, c0 in enumerate((0, 128, 192)):
            mm(A("PS", 512 * n, 512 * n + 128), A("QX", c0, c0 + 128), A("SX", c0, c0 + 128), A("QUP", 0, 128), A("SUP", 0, 128))
        if first:
            first()
        for n in range(3):
            h = 16 if n == 2 else 0
            for s in (0, 32):
                o = 8 * s + 32 * n
                tt(A("BT", o, o + 32 - h), A("PS", 512 * n + s + h, 512 * n + s + 32), A("THR", s + h, s + 32), OP.is_gt)
        quant("QB", 0, 192, A("BT", 0, 768))
        if second:
            second()
        for d in range(2):
            for i in range(2):
                k = 256 * d + 128 * i
                mm(A("PS", 1536 + 2048 * d, 1664 + 2048 * d), A("QK", k, k + 128), A("SK", k, k + 128), A("QB", 64 * i, 64 * i + 128), A("SB", 64 * i, 64 * i + 128), i == 0, i == 1)
        cp(A("KU0", 0, 20), A("PS", 1536, 1556))
        ts(d_(0, "KO"), A("PS", 1536, 1556), LW, OP.mult)
        act(A("KF0", 0, 320), IND(A("IDT", 0, 512), A("KU0", 0, 20)), scale=512.0)

    def back_signs():
        ts(A("KU1", 0, 20), A("PS", 3584, 3604), 7.0, OP.add)
        ts(d_(1, "KO"), A("PS", 3584, 3604), 7, OP.add, LW, OP.mult)
        act(A("KF1", 0, 320), IND(A("IDT", 0, 512), A("KU1", 0, 20)), scale=512.0)

    statics(0)
    quant("QU", 0, 128, A("UT", 0, 512))
    emit("v", V.tensor_copy, 1, CW("QUP", 0, 128), IND(CW("QU", 0, 128), A("UL", 0, 8)))
    act(A("SUP", 0, 128), IND(A("SU", 0, 128), A("UL", 0, 8)))
    quant("QK", 0, 512, A("KWT", 0, 2048))
    act(A("MF", 0, 320), A("IDT", 0, 320), scale=1025.0)

    def inverse2():
        emit("v", V.tensor_copy, 1, IND(A("QQ", 640, 960), A("LNU", 40, 60)), A("IDT", 0, 320))

    def columns():
        ts(A("ML", 0, 80), IND(A("QQ", 640, 960), A("CLU", 0, 5)), 320.0, OP.add)
        ts(A("ML", 80, 160), IND(A("QQ", 0, 320), A("CLU", 0, 5)), 320.0, OP.add)
        ts(A("ML", 160, 240), A("ML", 80, 160), 1024.0, OP.mult)
        tt(A("MF", 320, 400), A("ML", 160, 240), A("ML", 0, 80), OP.add)
        emit("v", V.tensor_copy, 1, IND(A("CF", 0, 400), A("PU", 0, 25)), A("MF", 0, 400))

    scores("R", inverse2, columns)
    tt(A("MG", 0, 400), A("CF", 0, 400), A("MASK", 0, 400), OP.mult)
    spread(A("SN", 0, 400), A("MG", 0, 400), 400)
    cp(ix(64, 89), A("SN", 15, 400, 16))
    ts(ix(96, 121), ix(64, 89), 1023, OP.bitwise_and)
    cp(A("CM0", 0, 25), ix(96, 121))

    def statics_back():
        tt(A("VA", 320, 640), IND(A("ID5", 0, 320), A("LNU", 40, 60)), A("IDT", 0, 320), OP.add)
        for i, (k, o) in enumerate(((20, 640), (0, 640), (0, 960))):
            ts(A("LOF1", 20 * i, 20 * i + 20), A("LN", k, k + 20), o, OP.add)
        emit("v", V.tensor_copy, 1, IND(A("QQ", 960, 1280), A("LNU", 20, 40)), A("VA", 320, 640))
        statics(1)
        ts(ix(96, 121), ix(64, 89), 10, OP.logical_shift_right)
        cp(A("CM1", 0, 25), ix(96, 121))
        tt(A("MG", 0, 80), A("ML", 80, 160), A("MASK", 0, 80), OP.mult)
        spread(A("SN", 0, 80), A("MG", 0, 80), 80)
        cp(A("LTL", 0, 5), A("SN", 15, 80, 16))
        quant("QV", 0, 128, A("VT", 0, 512))

    quant("QE", 0, 512, A("ET", 0, 2048))

    for r in range(STEPS):
        HQ, HS = "HQ%d" % r, "HS%d" % r
        peer = rank ^ MATES[r]
        n_arr = sum(mask_of(topo, T.cores[peer] if c is None else c, core)[1] for c in hops(T, topo, peer, r))
        arrives([A(HQ, 0, KX), A(HS, 0, KX)], "arr%d" % r, n_arr)
        if r:
            scores("XT")
        own = early(0)
        for f in own[:14]:
            f()
        gather_k(0)
        for f in own[14:]:
            f()
        late(0)
        lookup(0, "TN" if r else "T0", "FL0")
        offsets("OFZ", 0, "FL0", "CM0", C)
        pull("ZT", "OFZ", 0, 128)
        quant("QS", 0, 128, A("ZT", 0, 512))
        for k, c in enumerate(hops(T, topo, rank, r)):
            to = T.cores[peer] if c is None else c
            m, n = mask_of(topo, core, to)
            if k == 0:
                o = T[HQ if c is None else "QR"][:, 0:KX].bitcast(dt.uint8)
                i, rd = T.QS[:, 0:KX].bitcast(dt.uint8), [A("QS", 0, KX)]
            else:
                o = T[HS if c is None else "SR"][:, 0:KX]
                i, rd = T.SS[:, 0:KX], [A("SS", 0, KX)]
            remote(o, i, rd, "arr%d" % r if c is None else "rarr", "snt%d" % r, topo.addr(to, core), m, n)
        close("snt%d" % r)
        pull("ZT", "OFZ", 128, C)
        quant(HQ, KX, C, A("ZT", 4 * KX, 4 * C), HS)

        def layer(c0, c1, m1, buf, w, meanwhile=()):
            for b in range(4):
                for n, p in (("W", 0), ("E", 2048)):
                    mm(A("PS", p + 512 * b, p + 512 * b + m1), A("Q" + n, 128 * b, 128 * b + 128), A("S" + n, 128 * b, 128 * b + 128), A(HQ, c0, c0 + m1), A(HS, c0, c0 + m1))
            for b in range(4):
                l = A(buf, w * b, w * b + c1 - c0)
                act(l, A("PS", 512 * b, 512 * b + c1 - c0), RELU, scale=0.015625)
                k = 5 if b else 12
                for f in meanwhile[:k]:
                    f()
                meanwhile = meanwhile[k:]
                tt(A("R", 4 * c0 + b, 4 * c1, 4), l, A("PS", 2048 + 512 * b, 2048 + 512 * b + c1 - c0), OP.add)
            for f in meanwhile:
                f()

        back_signs()
        layer(KX, C, C - KX, "RL", 304, early(1) if r else [])
        shifted("d_ye%d" % r, "y", "R", 4 * C, T.R, 4 * KX, 4 * C, [A("R", 4 * KX, 4 * C)])
        if r == 0:
            statics_back()
            for f in early(1):
                f()
        gather_k(1)
        layer(0, KX, 128, "RL2", 128)
        shifted("d_yl%d" % r, "sy", "R", 4 * C, T.R, 0, 4 * KX, [A("R", 0, 4 * KX)])
        late(1)
        lookup(1, "T0", "FL1")
        cols = ST if r < STEPS - 1 else C
        offsets("OFX", 1, "FL1", "CM1", cols)
        if r < STEPS - 1:
            act(A("TN", 0, ST), A("FL1", 0, ST))
            act(A("TN", ST, C), IND(A("FL1", 0, 640), A("LTL", 0, 5)))
            shifted("d_tn%d" % r, "y", "TN", LW, T.TN, 0, C, [A("TN", 0, C)])
        else:
            lookup(0, "T0", "FLO", True)
            act(A("OPF", 0, C), IND(A("FLO", 0, 640), A("CM0", 0, 25)))
            for k in range(8):
                dma("y", "d_op", T.op[k:k + 1, :], T.OPF[16 * k:16 * k + 1, :], reads=[A("OPF", 0, C)])
            close("d_op")
        pull("XT", "OFX", 0, cols)

    quant("QX", 0, C, A("XT", 0, 4 * C))
    mm(A("PS", 0, C), A("QV", 0, 128), A("SV", 0, 128), A("QX", 0, C), A("SX", 0, C))
    dma("s", "d_out", T.oc[:, :], T.QX[:, :].bitcast(dt.uint8), reads=[A("QX", 0, C)])
    for k in range(4):
        dma("y", "d_out", T.osc[4 * k:4 * k + 4, :], T.SX[32 * k:32 * k + 4, :], reads=[A("SX", 0, C)])
    cp(A("YO", 0, C), A("PS", 0, C))
    dma("y", "d_out", T.y[:, :], T.YO[:, :], reads=[A("YO", 0, C)])
    close("d_out")
    finish()
